import numpy as np
import ml_dtypes


def mxq(x, axis, fmt="e4m3"):
    dtype, down = {"e4m3": (ml_dtypes.float8_e4m3fn, 7), "e5m2": (ml_dtypes.float8_e5m2, 14)}[fmt]
    v = np.moveaxis(np.asarray(x, np.float32).astype(ml_dtypes.bfloat16).astype(np.float64), axis, -1)
    blocks = v.reshape(v.shape[:-1] + (-1, 32))
    amax = np.abs(blocks).max(-1, keepdims=True)
    byte = np.maximum(np.where(amax > 0, np.frexp(amax)[1] - 1 + 127, 0) - down, 1)
    scale = np.exp2(byte - 127.0)
    codes = (blocks / scale).astype(np.float32).astype(dtype).astype(np.float64)
    return np.moveaxis((codes * scale).reshape(v.shape), -1, axis)


WIDE = False


def mx_kscale(k):
    if not WIDE:
        return np.ones(k)
    levels = np.array([10, -10, 5, -5, 0])
    if k % 512:
        return np.exp2(np.random.permutation(np.resize(levels, k // 32))).repeat(32)
    a = np.empty((k // 512, 16))
    for p in range(k // 512):
        a[p, :8] = np.random.permutation(np.resize(levels, 8))
        for g in range(8):
            far = levels[np.abs(levels - a[p, g]) >= 10]
            a[p, g + 8] = far[np.random.randint(len(far))]
    return np.exp2(a.ravel()).repeat(32)


def f64(x):
    return np.asarray(x).astype(np.float64)


def striped(idx):
    return np.tile(idx.reshape(-1, 16).T, (8, 1)).astype(np.uint16)


def unstriped(offs):
    return offs[:16].T.reshape(-1).astype(np.int64)


def pack_weight(w):
    k, n = w.shape
    w = f64(np.asarray(w, np.float32).astype(ml_dtypes.bfloat16)).reshape(k // 32, 32, n)
    amax = np.abs(w).max(1)
    byte = np.clip(np.where(amax > 0, np.frexp(amax)[1] - 1 + 127 - 7, 1), 1, 254)
    scaled = (w * np.exp2(127.0 - byte)[:, None, :]).reshape(k, n).astype(np.float32)
    words = np.ascontiguousarray(scaled.reshape(k // 512, 128, 4, n).transpose(0, 1, 3, 2)).astype(ml_dtypes.float8_e4m3fn).view(np.uint8)
    return words, np.ascontiguousarray(byte.astype(np.uint8).reshape(k // 512, 16, n))


def unpack_weight(words, scales):
    g, p, n, _ = words.shape
    vals = np.ascontiguousarray(words).view(ml_dtypes.float8_e4m3fn).astype(np.float64) * np.repeat(np.exp2(scales.astype(np.float64) - 127.0), 8, axis=1)[..., None]
    return vals.transpose(0, 1, 3, 2).reshape(g * 512, n)


K, T, S, D, H, N, V = 512, 1024, 512, 8, 512, 256, 64


def setup_inputs():
    n = np.random.standard_normal
    s = mx_kscale(K)[:, None]
    u = mx_kscale(H)
    packed_xT = pack_weight(n((K, T)) * s)
    return {
        "x_words": packed_xT[0],
        "x_scales": packed_xT[1],
        "w1": (n((K, H)) / np.sqrt(K) / s * u).astype(np.float32),
        "obs": (n((H, V)) * u[:, None]).astype(np.float32),
        "w2": (n((H, N)) / np.sqrt(H) / u[:, None]).astype(np.float32),
        "ens": (n((N, T))).astype(np.float32),
        "offs": striped(np.random.permutation(T)[:S]),
    }


def reference(x_words, x_scales, w1, obs, w2, ens, offs):
    xq = unpack_weight(x_words, x_scales)[:, unstriped(offs)]
    y = mxq(f64(w1), 0, "e4m3").T @ xq
    my = y.reshape(len(y), -1, D).mean(axis=2)
    om = f64(obs) - my
    rr = np.repeat(om, D, axis=1) - (0.3 * (y - np.repeat(my, D, axis=1)))
    return f64(ens)[:, unstriped(offs)] + (mxq(f64(w2), 0, "e4m3").T @ mxq(rr, 0, "e4m3"))

@@ -1,0 +1,144 @@
+import concourse.mybir as mybir
+
+K, T, S, D, H, N = 512, 1024, 512, 8, 512, 256
+V = S // D
+P = 128
+F32 = mybir.dt.float32
+BF16 = mybir.dt.bfloat16
+I32 = mybir.dt.int32
+U32 = mybir.dt.uint32
+U16 = mybir.dt.uint16
+U8 = mybir.dt.uint8
+X4 = mybir.dt.float8_e4m3fn_x4
+ALU = mybir.AluOpType
+ACT = mybir.ActivationFunctionType
+AX = mybir.AxisListType
+FLOPS = 2 * K * H * S + 2 * H * N * S
+CH = 128
+NCH = S // CH
+VC = CH // D
+
+
+def tile_picked_yenkf_third_p_kernel(tc, x_words, x_scales, w1, obs, w2, ens, offs, out):
+    nc = tc.nc
+    with (
+        tc.tile_pool(name="keep", bufs=1) as keep,
+        tc.psum_pool(name="psum", bufs=1) as psum,
+    ):
+        offsets = keep.tile([P, S // 16], U16, name="offsets")
+        nc.sync.dma_start(offsets[:], offs)
+
+        xs_all = keep.tile([P, T], U8, name="xs_all", align_bytes=64)
+        nc.vector.memset(xs_all[:].bitcast(I32), 0)
+        for q in range(4):
+            nc.scalar.dma_start(
+                xs_all[32 * q : 32 * q + 4, :].bitcast(I32),
+                x_scales[0, 4 * q : 4 * q + 4, :].bitcast(I32),
+            )
+
+        w1v = w1.rearrange("(p j) c -> p j c", j=4)
+        w1_raw = [keep.tile([P, 4, 256], F32, name="w1_raw%d" % h, align_bytes=64) for h in range(2)]
+        for h in range(2):
+            nc.sync.dma_start(w1_raw[h][:], w1v[:, :, 256 * h : 256 * (h + 1)])
+        xw_all = keep.tile([P, T], I32, name="xw_all", align_bytes=64)
+        nc.sync.dma_start(xw_all[:], x_words[0].rearrange("p n t -> p (n t)").bitcast(I32))
+        obs_sb = keep.tile([P, 4, V], F32, name="obs_sb", align_bytes=64)
+        nc.sync.dma_start(obs_sb[:], obs.rearrange("(p t) v -> p t v", t=4))
+        w2_raw = keep.tile([P, 4, N], F32, name="w2_raw", align_bytes=64)
+        nc.sync.dma_start(w2_raw[:], w2.rearrange("(p j) c -> p j c", j=4))
+        ens_sb = [keep.tile([P, T], F32, name="ens_sb%d" % a, align_bytes=64) for a in range(2)]
+        for a in range(2):
+            nc.sync.dma_start(ens_sb[a][:], ens[P * a : P * (a + 1), :])
+
+        xs = keep.tile([P, S], U8, name="xs", align_bytes=64)
+        nc.vector.tensor_copy(xs[:], xs_all[:].indirect(offsets[:]))
+
+        w1_g = keep.tile([P, 4, P, 4], BF16, name="w1_g", align_bytes=64)
+        for h in range(2):
+            dst = w1_g[:, :, 64 * h : 64 * (h + 1), :].rearrange("p t m j -> p m j t")
+            src = w1_raw[h][:].rearrange("p j (m t) -> p m j t", t=4)
+            if h == 0:
+                nc.scalar.copy(dst, src)
+            else:
+                nc.vector.tensor_copy(dst, src)
+        w1_c = keep.tile([P, H], U32, name="w1_c", align_bytes=64)
+        w1_s = keep.tile([P, H], U8, name="w1_s", align_bytes=64)
+        nc.vector.quantize_mx(out=w1_c[:].bitcast(X4), scales=w1_s[:], in_=w1_g[:].rearrange("p t m j -> p (t m j)"))
+
+        y = []
+        for c in range(NCH):
+            xw = keep.tile([P, CH], U32, name="xw%d" % c, align_bytes=64)
+            nc.vector.tensor_copy(xw[:], xw_all[:].bitcast(U32).indirect(offsets[:, 8 * c : 8 * (c + 1)]))
+            yc = psum.tile([P, 4, CH], F32, name="y%d" % c)
+            for t in range(4):
+                nc.tensor.matmul_mx(
+                    out=yc[:, t, :],
+                    lhsT=w1_c[:, P * t : P * (t + 1)].bitcast(X4),
+                    lhsT_scale=w1_s[:, P * t : P * (t + 1)],
+                    rhs=xw[:].bitcast(X4),
+                    rhs_scale=xs[:, CH * c : CH * (c + 1)],
+                    start=True,
+                    stop=True,
+                )
+            y.append(yc)
+
+        w2_g = keep.tile([P, N, 4], BF16, name="w2_g", align_bytes=64)
+        nc.scalar.copy(
+            w2_g[:].rearrange("p (c i) j -> p c j i", i=4),
+            w2_raw[:].rearrange("p j (c i) -> p c j i", i=4),
+        )
+        w2_c = keep.tile([P, N], U32, name="w2_c", align_bytes=64)
+        w2_s = keep.tile([P, N], U8, name="w2_s", align_bytes=64)
+        nc.vector.quantize_mx(out=w2_c[:].bitcast(X4), scales=w2_s[:], in_=w2_g[:].rearrange("p c j -> p (c j)"))
+
+        ens_g = keep.tile([P, 2, S], F32, name="ens_g", align_bytes=64)
+
+        sums, anom, cen, rr = [], [], [], []
+        for c in range(NCH):
+            sc = keep.tile([P, 4, VC], F32, name="sum%d" % c, align_bytes=64)
+            nc.vector.tensor_reduce(sc[:], y[c][:].rearrange("p t (v d) -> p t v d", d=D), AX.X, ALU.add)
+            ac = keep.tile([P, CH, 4], F32, name="anom%d" % c, align_bytes=64)
+            nc.scalar.activation(ac[:], y[c][:].rearrange("p t j -> p j t"), ACT.Copy, scale=-0.3)
+            sums.append(sc)
+            anom.append(ac)
+        for c in range(NCH):
+            cc = keep.tile([P, VC, 4], F32, name="cen%d" % c, align_bytes=64)
+            nc.vector.scalar_tensor_tensor(
+                cc[:],
+                sums[c][:].rearrange("p t v -> p v t"),
+                -0.7 / D,
+                obs_sb[:, :, VC * c : VC * (c + 1)].rearrange("p t v -> p v t"),
+                ALU.mult,
+                ALU.add,
+            )
+            cen.append(cc)
+        for c in range(NCH):
+            rc = keep.tile([P, CH * 4], BF16, name="rr%d" % c, align_bytes=64)
+            nc.vector.tensor_tensor(
+                rc[:].rearrange("p (v d t) -> p v d t", d=D, t=4),
+                anom[c][:].rearrange("p (v d) t -> p v d t", d=D),
+                cen[c][:].unsqueeze(2).to_broadcast([P, VC, D, 4]),
+                ALU.add,
+            )
+            rr.append(rc)
+        for a in range(2):
+            nc.vector.tensor_copy(ens_g[:, a, :], ens_sb[a][:].indirect(offsets[:]))
+        outv = out.rearrange("(a p) j -> p a j", p=P)
+        for c in range(NCH):
+            r_c = keep.tile([P, CH], U32, name="r_c%d" % c, align_bytes=64)
+            r_s = keep.tile([P, CH], U8, name="r_s%d" % c, align_bytes=64)
+            nc.vector.quantize_mx(out=r_c[:].bitcast(X4), scales=r_s[:], in_=rr[c][:])
+            z = psum.tile([P, 2, CH], F32, name="z%d" % c)
+            for a in range(2):
+                nc.tensor.matmul_mx(
+                    out=z[:, a, :],
+                    lhsT=w2_c[:, P * a : P * (a + 1)].bitcast(X4),
+                    lhsT_scale=w2_s[:, P * a : P * (a + 1)],
+                    rhs=r_c[:].bitcast(X4),
+                    rhs_scale=r_s[:],
+                    start=True,
+                    stop=True,
+                )
+            res = keep.tile([P, 2, CH], F32, name="res%d" % c, align_bytes=64)
+            nc.vector.tensor_tensor(res[:], z[:], ens_g[:, :, CH * c : CH * (c + 1)], ALU.add)
+            nc.sync.dma_start(outv[:, :, CH * c : CH * (c + 1)], res[:])

@@ -1,4 +1,5 @@
 import concourse.mybir as mybir
+from concourse.masks import make_identity
 
 K, T, S, D, H, N = 512, 1024, 512, 8, 512, 256
 V = S // D
@@ -12,11 +13,12 @@ U8 = mybir.dt.uint8
 X4 = mybir.dt.float8_e4m3fn_x4
 ALU = mybir.AluOpType
 ACT = mybir.ActivationFunctionType
-AX = mybir.AxisListType
 FLOPS = 2 * K * H * S + 2 * H * N * S
 CH = 128
 NCH = S // CH
 VC = CH // D
+GAIN = 0.3
+MEAN_FACTOR = (1.0 - GAIN) / (GAIN * D)
 
 
 def tile_picked_yenkf_third_p_kernel(tc, x_words, x_scales, w1, obs, w2, ens, offs, out):
@@ -29,11 +31,11 @@ def tile_picked_yenkf_third_p_kernel(tc, x_words, x_scales, w1, obs, w2, ens, of
         nc.sync.dma_start(offsets[:], offs)
 
         xs_all = keep.tile([P, T], U8, name="xs_all", align_bytes=64)
-        nc.vector.memset(xs_all[:].bitcast(I32), 0)
         for q in range(4):
-            nc.scalar.dma_start(
-                xs_all[32 * q : 32 * q + 4, :].bitcast(I32),
-                x_scales[0, 4 * q : 4 * q + 4, :].bitcast(I32),
+            queue = nc.sync if q < 2 else nc.scalar
+            queue.dma_start(
+                xs_all[32 * q : 32 * q + 32, :].bitcast(I32),
+                x_scales[0, 4 * q : 4 * q + 4, :].bitcast(I32).partition_broadcast(8),
             )
 
         w1v = w1.rearrange("(p j) c -> p j c", j=4)
@@ -44,94 +46,107 @@ def tile_picked_yenkf_third_p_kernel(tc, x_words, x_scales, w1, obs, w2, ens, of
         nc.sync.dma_start(xw_all[:], x_words[0].rearrange("p n t -> p (n t)").bitcast(I32))
         obs_sb = keep.tile([P, 4, V], F32, name="obs_sb", align_bytes=64)
         nc.sync.dma_start(obs_sb[:], obs.rearrange("(p t) v -> p t v", t=4))
-        w2_raw = keep.tile([P, 4, N], F32, name="w2_raw", align_bytes=64)
-        nc.sync.dma_start(w2_raw[:], w2.rearrange("(p j) c -> p j c", j=4))
         ens_sb = [keep.tile([P, T], F32, name="ens_sb%d" % a, align_bytes=64) for a in range(2)]
         for a in range(2):
             nc.sync.dma_start(ens_sb[a][:], ens[P * a : P * (a + 1), :])
+        w2_raw = keep.tile([P, 4, N], F32, name="w2_raw", align_bytes=64)
+        nc.sync.dma_start(w2_raw[:], w2.rearrange("(p j) c -> p j c", j=4))
+
+        ident = keep.tile([P, P], F32, name="ident", align_bytes=64)
+        make_identity(nc, ident[:])
 
         xs = keep.tile([P, S], U8, name="xs", align_bytes=64)
         nc.vector.tensor_copy(xs[:], xs_all[:].indirect(offsets[:]))
 
-        w1_g = keep.tile([P, 4, P, 4], BF16, name="w1_g", align_bytes=64)
+        w1_g = keep.tile([P, 4, P, 4], BF16, name="w1_g", tag="w1_g", align_bytes=64)
         for h in range(2):
-            dst = w1_g[:, :, 64 * h : 64 * (h + 1), :].rearrange("p t m j -> p m j t")
-            src = w1_raw[h][:].rearrange("p j (m t) -> p m j t", t=4)
-            if h == 0:
-                nc.scalar.copy(dst, src)
-            else:
-                nc.vector.tensor_copy(dst, src)
+            nc.vector.tensor_copy(
+                w1_g[:, :, 64 * h : 64 * (h + 1), :].rearrange("p t m j -> p m j t"),
+                w1_raw[h][:].rearrange("p j (m t) -> p m j t", t=4),
+            )
         w1_c = keep.tile([P, H], U32, name="w1_c", align_bytes=64)
         w1_s = keep.tile([P, H], U8, name="w1_s", align_bytes=64)
         nc.vector.quantize_mx(out=w1_c[:].bitcast(X4), scales=w1_s[:], in_=w1_g[:].rearrange("p t m j -> p (t m j)"))
 
-        y = []
+        anom = [keep.tile([P, D, 2 * VC, 4], F32, name="anom%d" % h, align_bytes=64) for h in range(2)]
+        xw = keep.tile([P, S], U32, name="xw", tag="w1_g", align_bytes=64)
         for c in range(NCH):
-            xw = keep.tile([P, CH], U32, name="xw%d" % c, align_bytes=64)
-            nc.vector.tensor_copy(xw[:], xw_all[:].bitcast(U32).indirect(offsets[:, 8 * c : 8 * (c + 1)]))
-            yc = psum.tile([P, 4, CH], F32, name="y%d" % c)
+            nc.vector.tensor_copy(xw[:, CH * c : CH * (c + 1)], xw_all[:].bitcast(U32).indirect(offsets[:, 8 * c : 8 * (c + 1)]))
+            yc = psum.tile([P, 4, CH], F32, name="y%d" % c, tag="bank%d" % c)
             for t in range(4):
                 nc.tensor.matmul_mx(
                     out=yc[:, t, :],
                     lhsT=w1_c[:, P * t : P * (t + 1)].bitcast(X4),
                     lhsT_scale=w1_s[:, P * t : P * (t + 1)],
-                    rhs=xw[:].bitcast(X4),
+                    rhs=xw[:, CH * c : CH * (c + 1)].bitcast(X4),
                     rhs_scale=xs[:, CH * c : CH * (c + 1)],
                     start=True,
                     stop=True,
                 )
-            y.append(yc)
+            nc.scalar.activation(
+                anom[c // 2][:, :, VC * (c % 2) : VC * (c % 2 + 1), :],
+                yc[:].rearrange("p t (v d) -> p d v t", d=D),
+                ACT.Copy,
+                scale=-GAIN,
+            )
+
+        obs_k = keep.tile([P, V, 4], F32, name="obs_k", align_bytes=64)
+        nc.gpsimd.tensor_scalar(
+            obs_k[:], obs_sb[:].rearrange("p t v -> p v t"), 1.0 / MEAN_FACTOR, 0.0, ALU.mult, ALU.add
+        )
+
+        ens_g = keep.tile([P, 2, S], F32, name="ens_g", align_bytes=64)
+        for a in range(2):
+            nc.vector.tensor_copy(ens_g[:, a, :], ens_sb[a][:].indirect(offsets[:]))
+
+        cen = []
+        for h in range(2):
+            turned = psum.tile([P, P], F32, name="turned%d" % h, tag="sum%d" % h)
+            terms = [anom[h][:, d, :, :] for d in range(D)] + [obs_k[:, 2 * VC * h : 2 * VC * (h + 1), :]]
+            for n, term in enumerate(terms):
+                nc.tensor.matmul(
+                    turned[:],
+                    term.rearrange("p v t -> p (v t)"),
+                    ident[:],
+                    start=(n == 0),
+                    stop=(n == D),
+                    is_transpose=True,
+                )
+            turned_sb = keep.tile([P, P], F32, name="turned_sb%d" % h, align_bytes=64)
+            nc.scalar.activation(turned_sb[:], turned[:], ACT.Copy, scale=MEAN_FACTOR)
+            ch = psum.tile([P, P], F32, name="cen%d" % h, tag="sum%d" % h)
+            nc.tensor.transpose(ch[:], turned_sb[:], ident[:])
+            cen.append(ch)
 
         w2_g = keep.tile([P, N, 4], BF16, name="w2_g", align_bytes=64)
-        nc.scalar.copy(
+        nc.vector.tensor_copy(
             w2_g[:].rearrange("p (c i) j -> p c j i", i=4),
             w2_raw[:].rearrange("p j (c i) -> p c j i", i=4),
         )
         w2_c = keep.tile([P, N], U32, name="w2_c", align_bytes=64)
         w2_s = keep.tile([P, N], U8, name="w2_s", align_bytes=64)
-        nc.vector.quantize_mx(out=w2_c[:].bitcast(X4), scales=w2_s[:], in_=w2_g[:].rearrange("p c j -> p (c j)"))
 
-        ens_g = keep.tile([P, 2, S], F32, name="ens_g", align_bytes=64)
-
-        sums, anom, cen, rr = [], [], [], []
-        for c in range(NCH):
-            sc = keep.tile([P, 4, VC], F32, name="sum%d" % c, align_bytes=64)
-            nc.vector.tensor_reduce(sc[:], y[c][:].rearrange("p t (v d) -> p t v d", d=D), AX.X, ALU.add)
-            ac = keep.tile([P, CH, 4], F32, name="anom%d" % c, align_bytes=64)
-            nc.scalar.activation(ac[:], y[c][:].rearrange("p t j -> p j t"), ACT.Copy, scale=-0.3)
-            sums.append(sc)
-            anom.append(ac)
-        for c in range(NCH):
-            cc = keep.tile([P, VC, 4], F32, name="cen%d" % c, align_bytes=64)
-            nc.vector.scalar_tensor_tensor(
-                cc[:],
-                sums[c][:].rearrange("p t v -> p v t"),
-                -0.7 / D,
-                obs_sb[:, :, VC * c : VC * (c + 1)].rearrange("p t v -> p v t"),
-                ALU.mult,
-                ALU.add,
-            )
-            cen.append(cc)
-        for c in range(NCH):
-            rc = keep.tile([P, CH * 4], BF16, name="rr%d" % c, align_bytes=64)
-            nc.vector.tensor_tensor(
-                rc[:].rearrange("p (v d t) -> p v d t", d=D, t=4),
-                anom[c][:].rearrange("p (v d) t -> p v d t", d=D),
-                cen[c][:].unsqueeze(2).to_broadcast([P, VC, D, 4]),
-                ALU.add,
-            )
-            rr.append(rc)
-        for a in range(2):
-            nc.vector.tensor_copy(ens_g[:, a, :], ens_sb[a][:].indirect(offsets[:]))
         outv = out.rearrange("(a p) j -> p a j", p=P)
-        for c in range(NCH):
+        rr, z = {}, {}
+
+        def combine(c):
+            h, w = c // 2, 4 * VC
+            rr[c] = keep.tile([P, D, w], BF16, name="rr%d" % c, align_bytes=64)
+            nc.vector.tensor_tensor(
+                rr[c][:],
+                anom[h][:].rearrange("p d v t -> p d (v t)")[:, :, w * (c % 2) : w * (c % 2 + 1)],
+                cen[h][:, w * (c % 2) : w * (c % 2 + 1)].unsqueeze(1).to_broadcast([P, D, w]),
+                ALU.add,
+            )
+
+        def product(c):
             r_c = keep.tile([P, CH], U32, name="r_c%d" % c, align_bytes=64)
             r_s = keep.tile([P, CH], U8, name="r_s%d" % c, align_bytes=64)
-            nc.vector.quantize_mx(out=r_c[:].bitcast(X4), scales=r_s[:], in_=rr[c][:])
-            z = psum.tile([P, 2, CH], F32, name="z%d" % c)
+            nc.vector.quantize_mx(out=r_c[:].bitcast(X4), scales=r_s[:], in_=rr[c][:].rearrange("p d w -> p (d w)"))
+            z[c] = psum.tile([P, 2, CH], F32, name="z%d" % c, tag="bank%d" % c)
             for a in range(2):
                 nc.tensor.matmul_mx(
-                    out=z[:, a, :],
+                    out=z[c][:, a, :],
                     lhsT=w2_c[:, P * a : P * (a + 1)].bitcast(X4),
                     lhsT_scale=w2_s[:, P * a : P * (a + 1)],
                     rhs=r_c[:].bitcast(X4),
@@ -139,6 +154,22 @@ def tile_picked_yenkf_third_p_kernel(tc, x_words, x_scales, w1, obs, w2, ens, of
                     start=True,
                     stop=True,
                 )
+
+        def finish(c):
             res = keep.tile([P, 2, CH], F32, name="res%d" % c, align_bytes=64)
-            nc.vector.tensor_tensor(res[:], z[:], ens_g[:, :, CH * c : CH * (c + 1)], ALU.add)
+            nc.vector.tensor_tensor(
+                res[:].rearrange("p a (v d) -> p a v d", d=D),
+                z[c][:].rearrange("p a (d v) -> p a v d", d=D),
+                ens_g[:, :, CH * c : CH * (c + 1)].rearrange("p a (v d) -> p a v d", d=D),
+                ALU.add,
+            )
             nc.sync.dma_start(outv[:, :, CH * c : CH * (c + 1)], res[:])
+
+        nc.vector.quantize_mx(out=w2_c[:].bitcast(X4), scales=w2_s[:], in_=w2_g[:].rearrange("p c j -> p (c j)"))
+        for step in range(NCH + 3):
+            if step < NCH:
+                combine(step)
+            if 1 <= step <= NCH:
+                product(step - 1)
+            if step >= 3:
+                finish(step - 3)

@@ -13,11 +13,13 @@ U8 = mybir.dt.uint8
 X4 = mybir.dt.float8_e4m3fn_x4
 ALU = mybir.AluOpType
 ACT = mybir.ActivationFunctionType
+AX = mybir.AxisListType
 FLOPS = 2 * K * H * S + 2 * H * N * S
 CH = 128
 NCH = S // CH
 VC = CH // D
 GAIN = 0.3
+W1_PIECES = ((0, 80), (80, 128))
 MEAN_FACTOR = (1.0 - GAIN) / (GAIN * D)
 
 
@@ -39,17 +41,19 @@ def tile_picked_yenkf_third_p_kernel(tc, x_words, x_scales, w1, obs, w2, ens, of
             )
 
         w1v = w1.rearrange("(p j) c -> p j c", j=4)
-        w1_raw = [keep.tile([P, 4, 256], F32, name="w1_raw%d" % h, align_bytes=64) for h in range(2)]
-        for h in range(2):
-            nc.sync.dma_start(w1_raw[h][:], w1v[:, :, 256 * h : 256 * (h + 1)])
+        w1_raw = []
+        for lo, hi in W1_PIECES:
+            raw = keep.tile([P, 4, 4 * (hi - lo)], F32, name="w1_raw%d" % lo, align_bytes=64)
+            nc.sync.dma_start(raw[:], w1v[:, :, 4 * lo : 4 * hi])
+            w1_raw.append(raw)
         xw_all = keep.tile([P, T], I32, name="xw_all", align_bytes=64)
         nc.sync.dma_start(xw_all[:], x_words[0].rearrange("p n t -> p (n t)").bitcast(I32))
         obs_sb = keep.tile([P, 4, V], F32, name="obs_sb", align_bytes=64)
         nc.sync.dma_start(obs_sb[:], obs.rearrange("(p t) v -> p t v", t=4))
         ens_sb = [keep.tile([P, T], F32, name="ens_sb%d" % a, align_bytes=64) for a in range(2)]
-        for a in range(2):
-            nc.sync.dma_start(ens_sb[a][:], ens[P * a : P * (a + 1), :])
         w2_raw = keep.tile([P, 4, N], F32, name="w2_raw", align_bytes=64)
+        nc.sync.dma_start(ens_sb[0][:], ens[0:P, :])
+        nc.sync.dma_start(ens_sb[1][:], ens[P : 2 * P, :])
         nc.sync.dma_start(w2_raw[:], w2.rearrange("(p j) c -> p j c", j=4))
 
         ident = keep.tile([P, P], F32, name="ident", align_bytes=64)
@@ -58,21 +62,40 @@ def tile_picked_yenkf_third_p_kernel(tc, x_words, x_scales, w1, obs, w2, ens, of
         xs = keep.tile([P, S], U8, name="xs", align_bytes=64)
         nc.vector.tensor_copy(xs[:], xs_all[:].indirect(offsets[:]))
 
-        w1_g = keep.tile([P, 4, P, 4], BF16, name="w1_g", tag="w1_g", align_bytes=64)
-        for h in range(2):
+        w1_g = keep.tile([P, 4, P, 4], BF16, name="w1_g", align_bytes=64)
+        for raw, (lo, hi) in zip(w1_raw, W1_PIECES):
             nc.vector.tensor_copy(
-                w1_g[:, :, 64 * h : 64 * (h + 1), :].rearrange("p t m j -> p m j t"),
-                w1_raw[h][:].rearrange("p j (m t) -> p m j t", t=4),
+                w1_g[:, :, lo:hi, :].rearrange("p t m j -> p m j t"),
+                raw[:].rearrange("p j (m t) -> p m j t", t=4),
             )
         w1_c = keep.tile([P, H], U32, name="w1_c", align_bytes=64)
         w1_s = keep.tile([P, H], U8, name="w1_s", align_bytes=64)
         nc.vector.quantize_mx(out=w1_c[:].bitcast(X4), scales=w1_s[:], in_=w1_g[:].rearrange("p t m j -> p (t m j)"))
 
-        anom = [keep.tile([P, D, 2 * VC, 4], F32, name="anom%d" % h, align_bytes=64) for h in range(2)]
-        xw = keep.tile([P, S], U32, name="xw", tag="w1_g", align_bytes=64)
+        W = 4 * VC
+        pair = keep.tile([P, D, 2 * W], F32, name="pair", align_bytes=64)
+        lone = keep.tile([P, (D + 2) * W], F32, name="lone", align_bytes=64)
+        last = keep.tile([P, D, W], F32, name="last", tag="last", align_bytes=64)
+        anom = [
+            pair[:, :, 0:W],
+            pair[:, :, W : 2 * W],
+            last[:],
+            lone[:, 0 : D * W].rearrange("p (d w) -> p d w", d=D),
+        ]
+        nc.gpsimd.memset(lone[:, (D + 1) * W :], 0.0)
+        obs_vt = obs_sb[:].rearrange("p t v -> p v t")
+        obs_pair = keep.tile([P, 2 * VC, 4], F32, name="obs_pair", align_bytes=64)
+        for dst, lo, hi in (
+            (obs_pair[:], 0, 2 * VC),
+            (lone[:, D * W : (D + 1) * W].rearrange("p (v t) -> p v t", t=4), 3 * VC, 4 * VC),
+        ):
+            nc.scalar.activation(dst, obs_vt[:, lo:hi, :], ACT.Copy, scale=1.0 / MEAN_FACTOR)
+        xw = keep.tile([P, S], U32, name="xw", align_bytes=64)
+        y = []
         for c in range(NCH):
             nc.vector.tensor_copy(xw[:, CH * c : CH * (c + 1)], xw_all[:].bitcast(U32).indirect(offsets[:, 8 * c : 8 * (c + 1)]))
             yc = psum.tile([P, 4, CH], F32, name="y%d" % c, tag="bank%d" % c)
+            y.append(yc)
             for t in range(4):
                 nc.tensor.matmul_mx(
                     out=yc[:, t, :],
@@ -84,42 +107,51 @@ def tile_picked_yenkf_third_p_kernel(tc, x_words, x_scales, w1, obs, w2, ens, of
                     stop=True,
                 )
             nc.scalar.activation(
-                anom[c // 2][:, :, VC * (c % 2) : VC * (c % 2 + 1), :],
+                anom[c].rearrange("p d (v t) -> p d v t", t=4),
                 yc[:].rearrange("p t (v d) -> p d v t", d=D),
                 ACT.Copy,
                 scale=-GAIN,
             )
 
-        obs_k = keep.tile([P, V, 4], F32, name="obs_k", align_bytes=64)
-        nc.gpsimd.tensor_scalar(
-            obs_k[:], obs_sb[:].rearrange("p t v -> p v t"), 1.0 / MEAN_FACTOR, 0.0, ALU.mult, ALU.add
-        )
-
         ens_g = keep.tile([P, 2, S], F32, name="ens_g", align_bytes=64)
         for a in range(2):
             nc.vector.tensor_copy(ens_g[:, a, :], ens_sb[a][:].indirect(offsets[:]))
+        sums = keep.tile([P, 4, VC], F32, name="sums", align_bytes=64)
+        nc.vector.tensor_reduce(sums[:], y[2][:].rearrange("p t (v d) -> p t v d", d=D), AX.X, ALU.add)
+        cen_last = keep.tile([P, VC, 4], F32, name="cen_last", align_bytes=64)
+        nc.vector.scalar_tensor_tensor(
+            cen_last[:],
+            sums[:].rearrange("p t v -> p v t"),
+            -(1.0 - GAIN) / D,
+            obs_vt[:, 2 * VC : 3 * VC, :],
+            ALU.mult,
+            ALU.add,
+        )
 
-        cen = []
-        for h in range(2):
+        centres = []
+        for h, terms in enumerate(
+            (
+                [pair[:, d, :] for d in range(D)] + [obs_pair[:].rearrange("p v t -> p (v t)")],
+                [lone[:, W * n : W * n + P] for n in range(D + 1)],
+            )
+        ):
             turned = psum.tile([P, P], F32, name="turned%d" % h, tag="sum%d" % h)
-            terms = [anom[h][:, d, :, :] for d in range(D)] + [obs_k[:, 2 * VC * h : 2 * VC * (h + 1), :]]
             for n, term in enumerate(terms):
-                nc.tensor.matmul(
-                    turned[:],
-                    term.rearrange("p v t -> p (v t)"),
-                    ident[:],
-                    start=(n == 0),
-                    stop=(n == D),
-                    is_transpose=True,
-                )
-            turned_sb = keep.tile([P, P], F32, name="turned_sb%d" % h, align_bytes=64)
+                nc.tensor.matmul(turned[:], term, ident[:], start=(n == 0), stop=(n == D), is_transpose=True)
+            turned_sb = keep.tile([P, P], F32, name="turned_sb%d" % h, tag="turned_sb%d" % h, align_bytes=64)
             nc.scalar.activation(turned_sb[:], turned[:], ACT.Copy, scale=MEAN_FACTOR)
-            ch = psum.tile([P, P], F32, name="cen%d" % h, tag="sum%d" % h)
-            nc.tensor.transpose(ch[:], turned_sb[:], ident[:])
-            cen.append(ch)
+            back = psum.tile([P, P], F32, name="back%d" % h, tag="sum%d" % h)
+            nc.tensor.transpose(back[:], turned_sb[:], ident[:])
+            centres.append(back)
+        cen = [
+            centres[0][:, 0:W],
+            centres[0][:, W : 2 * W],
+            cen_last[:].rearrange("p v t -> p (v t)"),
+            centres[1][:, 0:W],
+        ]
 
         w2_g = keep.tile([P, N, 4], BF16, name="w2_g", align_bytes=64)
-        nc.vector.tensor_copy(
+        nc.scalar.copy(
             w2_g[:].rearrange("p (c i) j -> p c j i", i=4),
             w2_raw[:].rearrange("p j (c i) -> p c j i", i=4),
         )
@@ -130,17 +162,11 @@ def tile_picked_yenkf_third_p_kernel(tc, x_words, x_scales, w1, obs, w2, ens, of
         rr, z = {}, {}
 
         def combine(c):
-            h, w = c // 2, 4 * VC
-            rr[c] = keep.tile([P, D, w], BF16, name="rr%d" % c, align_bytes=64)
-            nc.vector.tensor_tensor(
-                rr[c][:],
-                anom[h][:].rearrange("p d v t -> p d (v t)")[:, :, w * (c % 2) : w * (c % 2 + 1)],
-                cen[h][:, w * (c % 2) : w * (c % 2 + 1)].unsqueeze(1).to_broadcast([P, D, w]),
-                ALU.add,
-            )
+            rr[c] = keep.tile([P, D, W], BF16, name="rr%d" % c, tag="last" if c == 0 else "rr%d" % c, align_bytes=64)
+            nc.vector.tensor_tensor(rr[c][:], anom[c], cen[c].unsqueeze(1).to_broadcast([P, D, W]), ALU.add)
 
         def product(c):
-            r_c = keep.tile([P, CH], U32, name="r_c%d" % c, align_bytes=64)
+            r_c = keep.tile([P, CH], U32, name="r_c%d" % c, tag="turned_sb0" if c == 2 else "r_c%d" % c, align_bytes=64)
             r_s = keep.tile([P, CH], U8, name="r_s%d" % c, align_bytes=64)
             nc.vector.quantize_mx(out=r_c[:].bitcast(X4), scales=r_s[:], in_=rr[c][:].rearrange("p d w -> p (d w)"))
             z[c] = psum.tile([P, 2, CH], F32, name="z%d" % c, tag="bank%d" % c)
@@ -165,11 +191,15 @@ def tile_picked_yenkf_third_p_kernel(tc, x_words, x_scales, w1, obs, w2, ens, of
             )
             nc.sync.dma_start(outv[:, :, CH * c : CH * (c + 1)], res[:])
 
+        combine(2)
+        combine(0)
         nc.vector.quantize_mx(out=w2_c[:].bitcast(X4), scales=w2_s[:], in_=w2_g[:].rearrange("p c j -> p (c j)"))
-        for step in range(NCH + 3):
-            if step < NCH:
-                combine(step)
-            if 1 <= step <= NCH:
-                product(step - 1)
-            if step >= 3:
-                finish(step - 3)
+        product(2)
+        combine(1)
+        product(0)
+        combine(3)
+        product(1)
+        finish(2)
+        product(3)
+        for c in (0, 1, 3):
+            finish(c)

@@ -72,24 +72,26 @@ def tile_picked_yenkf_third_p_kernel(tc, x_words, x_scales, w1, obs, w2, ens, of
         w1_s = keep.tile([P, H], U8, name="w1_s", align_bytes=64)
         nc.vector.quantize_mx(out=w1_c[:].bitcast(X4), scales=w1_s[:], in_=w1_g[:].rearrange("p t m j -> p (t m j)"))
 
+        warm = psum.tile([P, H], F32, name="warm", tag="warm")
+        nc.tensor.matmul_mx(
+            out=warm[:],
+            lhsT=w1_c[:, 0:P].bitcast(X4),
+            lhsT_scale=w1_s[:, 0:P],
+            rhs=w1_c[:].bitcast(X4),
+            rhs_scale=w1_s[:],
+            start=True,
+            stop=True,
+        )
+
         W = 4 * VC
-        pair = keep.tile([P, D, 2 * W], F32, name="pair", align_bytes=64)
-        lone = keep.tile([P, (D + 2) * W], F32, name="lone", align_bytes=64)
-        last = keep.tile([P, D, W], F32, name="last", tag="last", align_bytes=64)
-        anom = [
-            pair[:, :, 0:W],
-            pair[:, :, W : 2 * W],
-            last[:],
-            lone[:, 0 : D * W].rearrange("p (d w) -> p d w", d=D),
-        ]
-        nc.gpsimd.memset(lone[:, (D + 1) * W :], 0.0)
+        pairs = [keep.tile([P, D, 2 * W], F32, name="pair%d" % h, tag="pair%d" % h, align_bytes=64) for h in range(2)]
+        anom = [pairs[c // 2][:, :, W * (c % 2) : W * (c % 2 + 1)] for c in range(NCH)]
         obs_vt = obs_sb[:].rearrange("p t v -> p v t")
-        obs_pair = keep.tile([P, 2 * VC, 4], F32, name="obs_pair", align_bytes=64)
-        for dst, lo, hi in (
-            (obs_pair[:], 0, 2 * VC),
-            (lone[:, D * W : (D + 1) * W].rearrange("p (v t) -> p v t", t=4), 3 * VC, 4 * VC),
-        ):
-            nc.scalar.activation(dst, obs_vt[:, lo:hi, :], ACT.Copy, scale=1.0 / MEAN_FACTOR)
+        obs_pair = []
+        for h in range(2):
+            scaled = keep.tile([P, 2 * VC, 4], F32, name="obs_pair%d" % h, tag="obs_pair%d" % h, align_bytes=64)
+            nc.scalar.activation(scaled[:], obs_vt[:, 2 * VC * h : 2 * VC * (h + 1), :], ACT.Copy, scale=1.0 / MEAN_FACTOR)
+            obs_pair.append(scaled)
         xw = keep.tile([P, S], U32, name="xw", align_bytes=64)
         y = []
         for c in range(NCH):
@@ -129,12 +131,8 @@ def tile_picked_yenkf_third_p_kernel(tc, x_words, x_scales, w1, obs, w2, ens, of
         )
 
         centres = []
-        for h, terms in enumerate(
-            (
-                [pair[:, d, :] for d in range(D)] + [obs_pair[:].rearrange("p v t -> p (v t)")],
-                [lone[:, W * n : W * n + P] for n in range(D + 1)],
-            )
-        ):
+        for h in range(2):
+            terms = [pairs[h][:, d, :] for d in range(D)] + [obs_pair[h][:].rearrange("p v t -> p (v t)")]
             turned = psum.tile([P, P], F32, name="turned%d" % h, tag="sum%d" % h)
             for n, term in enumerate(terms):
                 nc.tensor.matmul(turned[:], term, ident[:], start=(n == 0), stop=(n == D), is_transpose=True)
@@ -147,26 +145,34 @@ def tile_picked_yenkf_third_p_kernel(tc, x_words, x_scales, w1, obs, w2, ens, of
             centres[0][:, 0:W],
             centres[0][:, W : 2 * W],
             cen_last[:].rearrange("p v t -> p (v t)"),
-            centres[1][:, 0:W],
+            centres[1][:, W : 2 * W],
         ]
 
-        w2_g = keep.tile([P, N, 4], BF16, name="w2_g", align_bytes=64)
-        nc.scalar.copy(
-            w2_g[:].rearrange("p (c i) j -> p c j i", i=4),
-            w2_raw[:].rearrange("p j (c i) -> p c j i", i=4),
-        )
+        w2_g = []
+        for a in range(2):
+            half = keep.tile([P, P, 4], BF16, name="w2_g%d" % a, tag="obs_pair0" if a == 1 else "w2_g0", align_bytes=64)
+            nc.scalar.copy(
+                half[:].rearrange("p (c i) j -> p c j i", i=4),
+                w2_raw[:, :, P * a : P * (a + 1)].rearrange("p j (c i) -> p c j i", i=4),
+            )
+            w2_g.append(half)
         w2_c = keep.tile([P, N], U32, name="w2_c", align_bytes=64)
         w2_s = keep.tile([P, N], U8, name="w2_s", align_bytes=64)
 
         outv = out.rearrange("(a p) j -> p a j", p=P)
         rr, z = {}, {}
 
+        def quantise_w2(a):
+            cols = slice(P * a, P * (a + 1))
+            nc.vector.quantize_mx(out=w2_c[:, cols].bitcast(X4), scales=w2_s[:, cols], in_=w2_g[a][:].rearrange("p c j -> p (c j)"))
+
         def combine(c):
-            rr[c] = keep.tile([P, D, W], BF16, name="rr%d" % c, tag="last" if c == 0 else "rr%d" % c, align_bytes=64)
-            nc.vector.tensor_tensor(rr[c][:], anom[c], cen[c].unsqueeze(1).to_broadcast([P, D, W]), ALU.add)
+            rr[c] = keep.tile([P, D, W], BF16, name="rr%d" % c, align_bytes=64)
+            engine = nc.gpsimd if c == 2 else nc.vector
+            engine.tensor_tensor(rr[c][:], anom[c], cen[c].unsqueeze(1).to_broadcast([P, D, W]), ALU.add)
 
         def product(c):
-            r_c = keep.tile([P, CH], U32, name="r_c%d" % c, tag="turned_sb0" if c == 2 else "r_c%d" % c, align_bytes=64)
+            r_c = keep.tile([P, CH], U32, name="r_c%d" % c, tag="pair0" if c == 2 else "r_c%d" % c, align_bytes=64)
             r_s = keep.tile([P, CH], U8, name="r_s%d" % c, align_bytes=64)
             nc.vector.quantize_mx(out=r_c[:].bitcast(X4), scales=r_s[:], in_=rr[c][:].rearrange("p d w -> p (d w)"))
             z[c] = psum.tile([P, 2, CH], F32, name="z%d" % c, tag="bank%d" % c)
@@ -192,14 +198,12 @@ def tile_picked_yenkf_third_p_kernel(tc, x_words, x_scales, w1, obs, w2, ens, of
             nc.sync.dma_start(outv[:, :, CH * c : CH * (c + 1)], res[:])
 
         combine(2)
+        quantise_w2(0)
         combine(0)
-        nc.vector.quantize_mx(out=w2_c[:].bitcast(X4), scales=w2_s[:], in_=w2_g[:].rearrange("p c j -> p (c j)"))
-        product(2)
         combine(1)
-        product(0)
         combine(3)
-        product(1)
-        finish(2)
-        product(3)
-        for c in (0, 1, 3):
+        quantise_w2(1)
+        for c in range(NCH):
+            product(c)
+        for c in range(NCH):
             finish(c)

@@ -27,6 +27,7 @@ def tile_picked_yenkf_third_p_kernel(tc, x_words, x_scales, w1, obs, w2, ens, of
     nc = tc.nc
     with (
         tc.tile_pool(name="keep", bufs=1) as keep,
+        tc.tile_pool(name="turns", bufs=1) as turns,
         tc.psum_pool(name="psum", bufs=1) as psum,
     ):
         offsets = keep.tile([P, S // 16], U16, name="offsets")
@@ -89,9 +90,21 @@ def tile_picked_yenkf_third_p_kernel(tc, x_words, x_scales, w1, obs, w2, ens, of
         obs_vt = obs_sb[:].rearrange("p t v -> p v t")
         obs_pair = []
         for h in range(2):
-            scaled = keep.tile([P, 2 * VC, 4], F32, name="obs_pair%d" % h, tag="obs_pair%d" % h, align_bytes=64)
+            scaled = turns.tile([P, 2 * VC, 4], F32, name="obs_pair%d" % h, align_bytes=64, offset=(1024, 3072)[h])
             nc.scalar.activation(scaled[:], obs_vt[:, 2 * VC * h : 2 * VC * (h + 1), :], ACT.Copy, scale=1.0 / MEAN_FACTOR)
             obs_pair.append(scaled)
+        gain = turns.tile([P, 1], F32, name="gain", align_bytes=64, offset=448)
+        nc.gpsimd.memset(gain[:], 1.0)
+        nc.gpsimd.tensor_scalar(gain[:], gain[:], -GAIN, 0.0, ALU.mult, ALU.add)
+
+        def anomalies(c, lo, hi, scale):
+            nc.scalar.activation(
+                anom[c][:, lo:hi, :].rearrange("p d (v t) -> p d v t", t=4),
+                y[c][:].rearrange("p t (v d) -> p d v t", d=D)[:, lo:hi, :, :],
+                ACT.Copy,
+                scale=scale,
+            )
+
         xw = keep.tile([P, S], U32, name="xw", align_bytes=64)
         y = []
         for c in range(NCH):
@@ -108,18 +121,37 @@ def tile_picked_yenkf_third_p_kernel(tc, x_words, x_scales, w1, obs, w2, ens, of
                     start=True,
                     stop=True,
                 )
-            nc.scalar.activation(
-                anom[c].rearrange("p d (v t) -> p d v t", t=4),
-                yc[:].rearrange("p t (v d) -> p d v t", d=D),
-                ACT.Copy,
-                scale=-GAIN,
-            )
+            if c % 2 == 0:
+                anomalies(c, 0, D, -GAIN)
+            else:
+                anomalies(c, 0, D // 2, gain[:] if c == 3 else -GAIN)
+            if c == 1:
+                anomalies(c, D // 2, D, -GAIN)
 
-        ens_g = keep.tile([P, 2, S], F32, name="ens_g", align_bytes=64)
-        for a in range(2):
-            nc.vector.tensor_copy(ens_g[:, a, :], ens_sb[a][:].indirect(offsets[:]))
+        ens_early = keep.tile([P, 2, S], F32, name="ens_early", align_bytes=64)
+        nc.vector.tensor_copy(ens_early[:, 0, :], ens_sb[0][:].indirect(offsets[:]))
+        nc.vector.tensor_copy(ens_early[:, 1, 0 : S - CH], ens_sb[1][:].indirect(offsets[:, 0:24]))
         sums = keep.tile([P, 4, VC], F32, name="sums", align_bytes=64)
         nc.vector.tensor_reduce(sums[:], y[2][:].rearrange("p t (v d) -> p t v d", d=D), AX.X, ALU.add)
+
+        centres = []
+        for h in range(2):
+            members = [pairs[h][:, d, :] for d in range(D)]
+            observed = [obs_pair[h][:].rearrange("p v t -> p (v t)")]
+            terms = members + observed if h == 0 else observed + members
+            turned = psum.tile([P, P], F32, name="turned%d" % h, tag="sum%d" % h)
+            for n, term in enumerate(terms):
+                nc.tensor.matmul(turned[:], term, ident[:], start=(n == 0), stop=(n == D), is_transpose=True)
+            turned_sb = keep.tile([P, P], F32, name="turned_sb%d" % h, tag="turned_sb%d" % h, align_bytes=64)
+            nc.scalar.activation(turned_sb[:], turned[:], ACT.Copy, scale=MEAN_FACTOR)
+            if h == 0:
+                anomalies(3, D // 2, D, -GAIN)
+            back = psum.tile([P, P], F32, name="back%d" % h, tag="sum%d" % h)
+            nc.tensor.transpose(back[:], turned_sb[:], ident[:])
+            centres.append(back)
+        ens_late = turns.tile([P, CH], F32, name="ens_late", align_bytes=64, offset=0)
+        nc.vector.tensor_copy(ens_late[:], ens_sb[1][:].indirect(offsets[:, 24:32]))
+        ens_g = [ens_early[:, :, CH * c : CH * (c + 1)] for c in range(3)] + [(ens_early[:, 0, S - CH : S], ens_late[:])]
         cen_last = keep.tile([P, VC, 4], F32, name="cen_last", align_bytes=64)
         nc.vector.scalar_tensor_tensor(
             cen_last[:],
@@ -129,18 +161,6 @@ def tile_picked_yenkf_third_p_kernel(tc, x_words, x_scales, w1, obs, w2, ens, of
             ALU.mult,
             ALU.add,
         )
-
-        centres = []
-        for h in range(2):
-            terms = [pairs[h][:, d, :] for d in range(D)] + [obs_pair[h][:].rearrange("p v t -> p (v t)")]
-            turned = psum.tile([P, P], F32, name="turned%d" % h, tag="sum%d" % h)
-            for n, term in enumerate(terms):
-                nc.tensor.matmul(turned[:], term, ident[:], start=(n == 0), stop=(n == D), is_transpose=True)
-            turned_sb = keep.tile([P, P], F32, name="turned_sb%d" % h, tag="turned_sb%d" % h, align_bytes=64)
-            nc.scalar.activation(turned_sb[:], turned[:], ACT.Copy, scale=MEAN_FACTOR)
-            back = psum.tile([P, P], F32, name="back%d" % h, tag="sum%d" % h)
-            nc.tensor.transpose(back[:], turned_sb[:], ident[:])
-            centres.append(back)
         cen = [
             centres[0][:, 0:W],
             centres[0][:, W : 2 * W],
@@ -148,23 +168,16 @@ def tile_picked_yenkf_third_p_kernel(tc, x_words, x_scales, w1, obs, w2, ens, of
             centres[1][:, W : 2 * W],
         ]
 
-        w2_g = []
-        for a in range(2):
-            half = keep.tile([P, P, 4], BF16, name="w2_g%d" % a, tag="obs_pair0" if a == 1 else "w2_g0", align_bytes=64)
-            nc.scalar.copy(
-                half[:].rearrange("p (c i) j -> p c j i", i=4),
-                w2_raw[:, :, P * a : P * (a + 1)].rearrange("p j (c i) -> p c j i", i=4),
-            )
-            w2_g.append(half)
+        w2_g = turns.tile([P, N, 4], BF16, name="w2_g", align_bytes=64, offset=1024)
+        nc.scalar.copy(
+            w2_g[:].rearrange("p (c i) j -> p c j i", i=4),
+            w2_raw[:].rearrange("p j (c i) -> p c j i", i=4),
+        )
         w2_c = keep.tile([P, N], U32, name="w2_c", align_bytes=64)
         w2_s = keep.tile([P, N], U8, name="w2_s", align_bytes=64)
 
         outv = out.rearrange("(a p) j -> p a j", p=P)
         rr, z = {}, {}
-
-        def quantise_w2(a):
-            cols = slice(P * a, P * (a + 1))
-            nc.vector.quantize_mx(out=w2_c[:, cols].bitcast(X4), scales=w2_s[:, cols], in_=w2_g[a][:].rearrange("p c j -> p (c j)"))
 
         def combine(c):
             rr[c] = keep.tile([P, D, W], BF16, name="rr%d" % c, align_bytes=64)
@@ -175,10 +188,15 @@ def tile_picked_yenkf_third_p_kernel(tc, x_words, x_scales, w1, obs, w2, ens, of
             r_c = keep.tile([P, CH], U32, name="r_c%d" % c, tag="pair0" if c == 2 else "r_c%d" % c, align_bytes=64)
             r_s = keep.tile([P, CH], U8, name="r_s%d" % c, align_bytes=64)
             nc.vector.quantize_mx(out=r_c[:].bitcast(X4), scales=r_s[:], in_=rr[c][:].rearrange("p d w -> p (d w)"))
-            z[c] = psum.tile([P, 2, CH], F32, name="z%d" % c, tag="bank%d" % c)
+            if c == 3:
+                z[c] = [psum.tile([P, CH], F32, name="z3_%d" % a, tag=("bank3", "warm")[a])[:] for a in range(2)]
+                halves = z[c]
+            else:
+                z[c] = psum.tile([P, 2, CH], F32, name="z%d" % c, tag="bank%d" % c)
+                halves = [z[c][:, a, :] for a in range(2)]
             for a in range(2):
                 nc.tensor.matmul_mx(
-                    out=z[c][:, a, :],
+                    out=halves[a],
                     lhsT=w2_c[:, P * a : P * (a + 1)].bitcast(X4),
                     lhsT_scale=w2_s[:, P * a : P * (a + 1)],
                     rhs=r_c[:].bitcast(X4),
@@ -189,21 +207,31 @@ def tile_picked_yenkf_third_p_kernel(tc, x_words, x_scales, w1, obs, w2, ens, of
 
         def finish(c):
             res = keep.tile([P, 2, CH], F32, name="res%d" % c, align_bytes=64)
-            nc.vector.tensor_tensor(
-                res[:].rearrange("p a (v d) -> p a v d", d=D),
-                z[c][:].rearrange("p a (d v) -> p a v d", d=D),
-                ens_g[:, :, CH * c : CH * (c + 1)].rearrange("p a (v d) -> p a v d", d=D),
-                ALU.add,
-            )
+            if c == 3:
+                for a in range(2):
+                    nc.vector.tensor_tensor(
+                        res[:, a, :].rearrange("p (v d) -> p v d", d=D),
+                        z[c][a].rearrange("p (d v) -> p v d", d=D),
+                        ens_g[c][a].rearrange("p (v d) -> p v d", d=D),
+                        ALU.add,
+                    )
+            else:
+                nc.vector.tensor_tensor(
+                    res[:].rearrange("p a (v d) -> p a v d", d=D),
+                    z[c][:].rearrange("p a (d v) -> p a v d", d=D),
+                    ens_g[c].rearrange("p a (v d) -> p a v d", d=D),
+                    ALU.add,
+                )
             nc.sync.dma_start(outv[:, :, CH * c : CH * (c + 1)], res[:])
 
         combine(2)
-        quantise_w2(0)
         combine(0)
         combine(1)
-        combine(3)
-        quantise_w2(1)
-        for c in range(NCH):
+        nc.vector.quantize_mx(out=w2_c[:].bitcast(X4), scales=w2_s[:], in_=w2_g[:].rearrange("p c j -> p (c j)"))
+        for c in range(3):
             product(c)
-        for c in range(NCH):
+        combine(3)
+        finish(0)
+        product(3)
+        for c in (1, 2, 3):
             finish(c)

@@ -71,18 +71,25 @@ def tile_picked_yenkf_third_p_kernel(tc, x_words, x_scales, w1, obs, w2, ens, of
             )
         w1_c = keep.tile([P, H], U32, name="w1_c", align_bytes=64)
         w1_s = keep.tile([P, H], U8, name="w1_s", align_bytes=64)
-        nc.vector.quantize_mx(out=w1_c[:].bitcast(X4), scales=w1_s[:], in_=w1_g[:].rearrange("p t m j -> p (t m j)"))
+        for h in range(2):
+            cols = slice(2 * P * h, 2 * P * (h + 1))
+            nc.vector.quantize_mx(
+                out=w1_c[:, cols].bitcast(X4),
+                scales=w1_s[:, cols],
+                in_=w1_g[:, 2 * h : 2 * h + 2, :, :].rearrange("p t m j -> p (t m j)"),
+            )
 
-        warm = psum.tile([P, H], F32, name="warm", tag="warm")
-        nc.tensor.matmul_mx(
-            out=warm[:],
-            lhsT=w1_c[:, 0:P].bitcast(X4),
-            lhsT_scale=w1_s[:, 0:P],
-            rhs=w1_c[:].bitcast(X4),
-            rhs_scale=w1_s[:],
-            start=True,
-            stop=True,
-        )
+        warm = psum.tile([P, 2, 2 * P], F32, name="warm", tag="warm")
+        for n in range(3):
+            nc.tensor.matmul_mx(
+                out=warm[:, n % 2, :],
+                lhsT=w1_c[:, 0:P].bitcast(X4),
+                lhsT_scale=w1_s[:, 0:P],
+                rhs=w1_c[:, 0 : 2 * P].bitcast(X4),
+                rhs_scale=w1_s[:, 0 : 2 * P],
+                start=True,
+                stop=True,
+            )
 
         W = 4 * VC
         pairs = [keep.tile([P, D, 2 * W], F32, name="pair%d" % h, tag="pair%d" % h, align_bytes=64) for h in range(2)]
@@ -108,7 +115,9 @@ def tile_picked_yenkf_third_p_kernel(tc, x_words, x_scales, w1, obs, w2, ens, of
         xw = keep.tile([P, S], U32, name="xw", align_bytes=64)
         y = []
         for c in range(NCH):
-            nc.vector.tensor_copy(xw[:, CH * c : CH * (c + 1)], xw_all[:].bitcast(U32).indirect(offsets[:, 8 * c : 8 * (c + 1)]))
+            if c < 3:
+                last = c + 1 if c < 2 else NCH
+                nc.vector.tensor_copy(xw[:, CH * c : CH * last], xw_all[:].bitcast(U32).indirect(offsets[:, 8 * c : 8 * last]))
             yc = psum.tile([P, 4, CH], F32, name="y%d" % c, tag="bank%d" % c)
             y.append(yc)
             for t in range(4):
@@ -138,7 +147,7 @@ def tile_picked_yenkf_third_p_kernel(tc, x_words, x_scales, w1, obs, w2, ens, of
         for h in range(2):
             members = [pairs[h][:, d, :] for d in range(D)]
             observed = [obs_pair[h][:].rearrange("p v t -> p (v t)")]
-            terms = members + observed if h == 0 else observed + members
+            terms = members + observed
             turned = psum.tile([P, P], F32, name="turned%d" % h, tag="sum%d" % h)
             for n, term in enumerate(terms):
                 nc.tensor.matmul(turned[:], term, ident[:], start=(n == 0), stop=(n == D), is_transpose=True)

@@ -71,25 +71,8 @@ def tile_picked_yenkf_third_p_kernel(tc, x_words, x_scales, w1, obs, w2, ens, of
             )
         w1_c = keep.tile([P, H], U32, name="w1_c", align_bytes=64)
         w1_s = keep.tile([P, H], U8, name="w1_s", align_bytes=64)
-        for h in range(2):
-            cols = slice(2 * P * h, 2 * P * (h + 1))
-            nc.vector.quantize_mx(
-                out=w1_c[:, cols].bitcast(X4),
-                scales=w1_s[:, cols],
-                in_=w1_g[:, 2 * h : 2 * h + 2, :, :].rearrange("p t m j -> p (t m j)"),
-            )
+        nc.vector.quantize_mx(out=w1_c[:].bitcast(X4), scales=w1_s[:], in_=w1_g[:].rearrange("p t m j -> p (t m j)"))
 
-        warm = psum.tile([P, 2, 2 * P], F32, name="warm", tag="warm")
-        for n in range(3):
-            nc.tensor.matmul_mx(
-                out=warm[:, n % 2, :],
-                lhsT=w1_c[:, 0:P].bitcast(X4),
-                lhsT_scale=w1_s[:, 0:P],
-                rhs=w1_c[:, 0 : 2 * P].bitcast(X4),
-                rhs_scale=w1_s[:, 0 : 2 * P],
-                start=True,
-                stop=True,
-            )
 
         W = 4 * VC
         pairs = [keep.tile([P, D, 2 * W], F32, name="pair%d" % h, tag="pair%d" % h, align_bytes=64) for h in range(2)]

@@ -63,16 +63,18 @@ def tile_picked_yenkf_third_p_kernel(tc, x_words, x_scales, w1, obs, w2, ens, of
         xs = keep.tile([P, S], U8, name="xs", align_bytes=64)
         nc.vector.tensor_copy(xs[:], xs_all[:].indirect(offsets[:]))
 
-        w1_g = keep.tile([P, 4, P, 4], BF16, name="w1_g", align_bytes=64)
+        w1_g = [keep.tile([P, 2, P, 4], BF16, name="w1_g%d" % u, tag="w1_g%d" % u, align_bytes=64) for u in range(2)]
         for raw, (lo, hi) in zip(w1_raw, W1_PIECES):
-            nc.vector.tensor_copy(
-                w1_g[:, :, lo:hi, :].rearrange("p t m j -> p m j t"),
-                raw[:].rearrange("p j (m t) -> p m j t", t=4),
-            )
+            for u, copy in enumerate((nc.vector.tensor_copy, nc.scalar.copy)):
+                copy(
+                    w1_g[u][:, :, lo:hi, :].rearrange("p t m j -> p m j t"),
+                    raw[:].rearrange("p j (m t) -> p m j t", t=4)[:, :, :, 2 * u : 2 * u + 2],
+                )
         w1_c = keep.tile([P, H], U32, name="w1_c", align_bytes=64)
         w1_s = keep.tile([P, H], U8, name="w1_s", align_bytes=64)
-        nc.vector.quantize_mx(out=w1_c[:].bitcast(X4), scales=w1_s[:], in_=w1_g[:].rearrange("p t m j -> p (t m j)"))
-
+        for u in range(2):
+            cols = slice(H // 2 * u, H // 2 * (u + 1))
+            nc.vector.quantize_mx(out=w1_c[:, cols].bitcast(X4), scales=w1_s[:, cols], in_=w1_g[u][:].rearrange("p t m j -> p (t m j)"))
 
         W = 4 * VC
         pairs = [keep.tile([P, D, 2 * W], F32, name="pair%d" % h, tag="pair%d" % h, align_bytes=64) for h in range(2)]
@@ -95,7 +97,7 @@ def tile_picked_yenkf_third_p_kernel(tc, x_words, x_scales, w1, obs, w2, ens, of
                 scale=scale,
             )
 
-        xw = keep.tile([P, S], U32, name="xw", align_bytes=64)
+        xw = keep.tile([P, S], U32, name="xw", tag="w1_g1", align_bytes=64)
         y = []
         for c in range(NCH):
             if c < 3:

@@ -19,7 +19,7 @@ CH = 128
 NCH = S // CH
 VC = CH // D
 GAIN = 0.3
-W1_PIECES = ((0, 80), (80, 128))
+W1_PIECES = ((0, 48), (48, 128))
 MEAN_FACTOR = (1.0 - GAIN) / (GAIN * D)
 
 
@@ -34,12 +34,7 @@ def tile_picked_yenkf_third_p_kernel(tc, x_words, x_scales, w1, obs, w2, ens, of
         nc.sync.dma_start(offsets[:], offs)
 
         xs_all = keep.tile([P, T], U8, name="xs_all", align_bytes=64)
-        for q in range(4):
-            queue = nc.sync if q < 2 else nc.scalar
-            queue.dma_start(
-                xs_all[32 * q : 32 * q + 32, :].bitcast(I32),
-                x_scales[0, 4 * q : 4 * q + 4, :].bitcast(I32).partition_broadcast(8),
-            )
+        nc.vector.memset(xs_all[:].bitcast(I32), 0)
 
         w1v = w1.rearrange("(p j) c -> p j c", j=4)
         w1_raw = []
@@ -47,14 +42,17 @@ def tile_picked_yenkf_third_p_kernel(tc, x_words, x_scales, w1, obs, w2, ens, of
             raw = keep.tile([P, 4, 4 * (hi - lo)], F32, name="w1_raw%d" % lo, align_bytes=64)
             nc.sync.dma_start(raw[:], w1v[:, :, 4 * lo : 4 * hi])
             w1_raw.append(raw)
+            if lo == 0:
+                for q in range(4):
+                    nc.sync.dma_start(xs_all[32 * q : 32 * q + 4, :].bitcast(I32), x_scales[0, 4 * q : 4 * q + 4, :].bitcast(I32))
         xw_all = keep.tile([P, T], I32, name="xw_all", align_bytes=64)
         nc.sync.dma_start(xw_all[:], x_words[0].rearrange("p n t -> p (n t)").bitcast(I32))
         obs_sb = keep.tile([P, 4, V], F32, name="obs_sb", align_bytes=64)
-        nc.sync.dma_start(obs_sb[:], obs.rearrange("(p t) v -> p t v", t=4))
         ens_sb = [keep.tile([P, T], F32, name="ens_sb%d" % a, align_bytes=64) for a in range(2)]
         w2_raw = keep.tile([P, 4, N], F32, name="w2_raw", align_bytes=64)
         nc.sync.dma_start(ens_sb[0][:], ens[0:P, :])
         nc.sync.dma_start(ens_sb[1][:], ens[P : 2 * P, :])
+        nc.sync.dma_start(obs_sb[:], obs.rearrange("(p t) v -> p t v", t=4))
         nc.sync.dma_start(w2_raw[:], w2.rearrange("(p j) c -> p j c", j=4))
 
         ident = keep.tile([P, P], F32, name="ident", align_bytes=64)
@@ -65,7 +63,8 @@ def tile_picked_yenkf_third_p_kernel(tc, x_words, x_scales, w1, obs, w2, ens, of
 
         w1_g = [keep.tile([P, 2, P, 4], BF16, name="w1_g%d" % u, tag="w1_g%d" % u, align_bytes=64) for u in range(2)]
         for raw, (lo, hi) in zip(w1_raw, W1_PIECES):
-            for u, copy in enumerate((nc.vector.tensor_copy, nc.scalar.copy)):
+            for u in range(2):
+                copy = nc.vector.tensor_copy if lo > 0 and u == 0 else nc.scalar.copy
                 copy(
                     w1_g[u][:, :, lo:hi, :].rearrange("p t m j -> p m j t"),
                     raw[:].rearrange("p j (m t) -> p m j t", t=4)[:, :, :, 2 * u : 2 * u + 2],
@@ -83,11 +82,15 @@ def tile_picked_yenkf_third_p_kernel(tc, x_words, x_scales, w1, obs, w2, ens, of
         obs_pair = []
         for h in range(2):
             scaled = turns.tile([P, 2 * VC, 4], F32, name="obs_pair%d" % h, align_bytes=64, offset=(1024, 3072)[h])
-            nc.scalar.activation(scaled[:], obs_vt[:, 2 * VC * h : 2 * VC * (h + 1), :], ACT.Copy, scale=1.0 / MEAN_FACTOR)
+            nc.gpsimd.tensor_scalar(scaled[:], obs_vt[:, 2 * VC * h : 2 * VC * (h + 1), :], 1.0 / MEAN_FACTOR, 0.0, ALU.mult, ALU.add)
             obs_pair.append(scaled)
         gain = turns.tile([P, 1], F32, name="gain", align_bytes=64, offset=448)
         nc.gpsimd.memset(gain[:], 1.0)
         nc.gpsimd.tensor_scalar(gain[:], gain[:], -GAIN, 0.0, ALU.mult, ALU.add)
+
+        mean_factor = keep.tile([P, 1], F32, name="mean_factor", tag="mean_factor", align_bytes=64)
+        nc.gpsimd.memset(mean_factor[:], 1.0)
+        nc.gpsimd.tensor_scalar(mean_factor[:], mean_factor[:], MEAN_FACTOR, 0.0, ALU.mult, ALU.add)
 
         def anomalies(c, lo, hi, scale):
             nc.scalar.activation(
@@ -132,12 +135,12 @@ def tile_picked_yenkf_third_p_kernel(tc, x_words, x_scales, w1, obs, w2, ens, of
         for h in range(2):
             members = [pairs[h][:, d, :] for d in range(D)]
             observed = [obs_pair[h][:].rearrange("p v t -> p (v t)")]
-            terms = members + observed
+            terms = observed + members
             turned = psum.tile([P, P], F32, name="turned%d" % h, tag="sum%d" % h)
             for n, term in enumerate(terms):
                 nc.tensor.matmul(turned[:], term, ident[:], start=(n == 0), stop=(n == D), is_transpose=True)
             turned_sb = keep.tile([P, P], F32, name="turned_sb%d" % h, tag="turned_sb%d" % h, align_bytes=64)
-            nc.scalar.activation(turned_sb[:], turned[:], ACT.Copy, scale=MEAN_FACTOR)
+            nc.scalar.activation(turned_sb[:], turned[:], ACT.Copy, scale=mean_factor[:] if h == 0 else MEAN_FACTOR)
             if h == 0:
                 anomalies(3, D // 2, D, -GAIN)
             back = psum.tile([P, P], F32, name="back%d" % h, tag="sum%d" % h)
@@ -162,7 +165,7 @@ def tile_picked_yenkf_third_p_kernel(tc, x_words, x_scales, w1, obs, w2, ens, of
             centres[1][:, W : 2 * W],
         ]
 
-        w2_g = turns.tile([P, N, 4], BF16, name="w2_g", align_bytes=64, offset=1024)
+        w2_g = keep.tile([P, N, 4], BF16, name="w2_g", tag="mean_factor", align_bytes=64)
         nc.scalar.copy(
             w2_g[:].rearrange("p (c i) j -> p c j i", i=4),
             w2_raw[:].rearrange("p j (c i) -> p c j i", i=4),

@@ -19,7 +19,7 @@ CH = 128
 NCH = S // CH
 VC = CH // D
 GAIN = 0.3
-W1_PIECES = ((0, 48), (48, 128))
+W1_PIECES = ((0, 64), (64, 128))
 MEAN_FACTOR = (1.0 - GAIN) / (GAIN * D)
 
 
@@ -31,7 +31,6 @@ def tile_picked_yenkf_third_p_kernel(tc, x_words, x_scales, w1, obs, w2, ens, of
         tc.psum_pool(name="psum", bufs=1) as psum,
     ):
         offsets = keep.tile([P, S // 16], U16, name="offsets")
-        nc.sync.dma_start(offsets[:], offs)
 
         xs_all = keep.tile([P, T], U8, name="xs_all", align_bytes=64)
         nc.vector.memset(xs_all[:].bitcast(I32), 0)
@@ -43,6 +42,7 @@ def tile_picked_yenkf_third_p_kernel(tc, x_words, x_scales, w1, obs, w2, ens, of
             nc.sync.dma_start(raw[:], w1v[:, :, 4 * lo : 4 * hi])
             w1_raw.append(raw)
             if lo == 0:
+                nc.sync.dma_start(offsets[:], offs)
                 for q in range(4):
                     nc.sync.dma_start(xs_all[32 * q : 32 * q + 4, :].bitcast(I32), x_scales[0, 4 * q : 4 * q + 4, :].bitcast(I32))
         xw_all = keep.tile([P, T], I32, name="xw_all", align_bytes=64)

@@ -20,6 +20,7 @@ NCH = S // CH
 VC = CH // D
 GAIN = 0.3
 W1_PIECES = ((0, 64), (64, 128))
+SHARED = 5
 MEAN_FACTOR = (1.0 - GAIN) / (GAIN * D)
 
 
@@ -27,7 +28,6 @@ def tile_picked_yenkf_third_p_kernel(tc, x_words, x_scales, w1, obs, w2, ens, of
     nc = tc.nc
     with (
         tc.tile_pool(name="keep", bufs=1) as keep,
-        tc.tile_pool(name="turns", bufs=1) as turns,
         tc.psum_pool(name="psum", bufs=1) as psum,
     ):
         offsets = keep.tile([P, S // 16], U16, name="offsets")
@@ -50,10 +50,10 @@ def tile_picked_yenkf_third_p_kernel(tc, x_words, x_scales, w1, obs, w2, ens, of
         obs_sb = keep.tile([P, 4, V], F32, name="obs_sb", align_bytes=64)
         ens_sb = [keep.tile([P, T], F32, name="ens_sb%d" % a, align_bytes=64) for a in range(2)]
         w2_raw = keep.tile([P, 4, N], F32, name="w2_raw", align_bytes=64)
+        nc.sync.dma_start(w2_raw[:], w2.rearrange("(p j) c -> p j c", j=4))
+        nc.sync.dma_start(obs_sb[:], obs.rearrange("(p t) v -> p t v", t=4))
         nc.sync.dma_start(ens_sb[0][:], ens[0:P, :])
         nc.sync.dma_start(ens_sb[1][:], ens[P : 2 * P, :])
-        nc.sync.dma_start(obs_sb[:], obs.rearrange("(p t) v -> p t v", t=4))
-        nc.sync.dma_start(w2_raw[:], w2.rearrange("(p j) c -> p j c", j=4))
 
         ident = keep.tile([P, P], F32, name="ident", align_bytes=64)
         make_identity(nc, ident[:])
@@ -76,28 +76,24 @@ def tile_picked_yenkf_third_p_kernel(tc, x_words, x_scales, w1, obs, w2, ens, of
             nc.vector.quantize_mx(out=w1_c[:, cols].bitcast(X4), scales=w1_s[:, cols], in_=w1_g[u][:].rearrange("p t m j -> p (t m j)"))
 
         W = 4 * VC
-        pairs = [keep.tile([P, D, 2 * W], F32, name="pair%d" % h, tag="pair%d" % h, align_bytes=64) for h in range(2)]
-        anom = [pairs[c // 2][:, :, W * (c % 2) : W * (c % 2 + 1)] for c in range(NCH)]
+        pair = keep.tile([P, D, 2 * W], F32, name="pair", align_bytes=64)
+        anom_last = keep.tile([P, D, W], F32, name="anom_last", align_bytes=64)
+        anom_first = keep.tile([P, SHARED, W], F32, name="anom_first", align_bytes=64)
+        anom = {0: anom_first[:], 1: pair[:, :, 0:W], 2: pair[:, :, W : 2 * W], 3: anom_last[:]}
         obs_vt = obs_sb[:].rearrange("p t v -> p v t")
-        obs_pair = []
-        for h in range(2):
-            scaled = turns.tile([P, 2 * VC, 4], F32, name="obs_pair%d" % h, align_bytes=64, offset=(1024, 3072)[h])
-            nc.gpsimd.tensor_scalar(scaled[:], obs_vt[:, 2 * VC * h : 2 * VC * (h + 1), :], 1.0 / MEAN_FACTOR, 0.0, ALU.mult, ALU.add)
-            obs_pair.append(scaled)
-        gain = turns.tile([P, 1], F32, name="gain", align_bytes=64, offset=448)
-        nc.gpsimd.memset(gain[:], 1.0)
-        nc.gpsimd.tensor_scalar(gain[:], gain[:], -GAIN, 0.0, ALU.mult, ALU.add)
+        obs_pair = keep.tile([P, 2 * VC, 4], F32, name="obs_pair", align_bytes=64)
+        nc.gpsimd.tensor_scalar(obs_pair[:], obs_vt[:, VC : 3 * VC, :], 1.0 / MEAN_FACTOR, 0.0, ALU.mult, ALU.add)
 
         mean_factor = keep.tile([P, 1], F32, name="mean_factor", tag="mean_factor", align_bytes=64)
         nc.gpsimd.memset(mean_factor[:], 1.0)
         nc.gpsimd.tensor_scalar(mean_factor[:], mean_factor[:], MEAN_FACTOR, 0.0, ALU.mult, ALU.add)
 
-        def anomalies(c, lo, hi, scale):
+        def anomalies(c, lo, hi):
             nc.scalar.activation(
                 anom[c][:, lo:hi, :].rearrange("p d (v t) -> p d v t", t=4),
                 y[c][:].rearrange("p t (v d) -> p d v t", d=D)[:, lo:hi, :, :],
                 ACT.Copy,
-                scale=scale,
+                scale=-GAIN,
             )
 
         xw = keep.tile([P, S], U32, name="xw", tag="w1_g1", align_bytes=64)
@@ -118,58 +114,46 @@ def tile_picked_yenkf_third_p_kernel(tc, x_words, x_scales, w1, obs, w2, ens, of
                     start=True,
                     stop=True,
                 )
-            if c % 2 == 0:
-                anomalies(c, 0, D, -GAIN)
+            if c == 2:
+                anomalies(c, 0, D // 2)
+                anomalies(c, D // 2, D)
             else:
-                anomalies(c, 0, D // 2, gain[:] if c == 3 else -GAIN)
-            if c == 1:
-                anomalies(c, D // 2, D, -GAIN)
+                anomalies(c, 0, D if c > 0 else SHARED)
 
-        ens_early = keep.tile([P, 2, S], F32, name="ens_early", align_bytes=64)
-        nc.vector.tensor_copy(ens_early[:, 0, :], ens_sb[0][:].indirect(offsets[:]))
-        nc.vector.tensor_copy(ens_early[:, 1, 0 : S - CH], ens_sb[1][:].indirect(offsets[:, 0:24]))
-        sums = keep.tile([P, 4, VC], F32, name="sums", align_bytes=64)
-        nc.vector.tensor_reduce(sums[:], y[2][:].rearrange("p t (v d) -> p t v d", d=D), AX.X, ALU.add)
+        ens_first = keep.tile([P, CH], F32, name="ens_first", align_bytes=64)
+        nc.scalar.activation(ens_first[:], ens_sb[0][:].indirect(offsets[:, 0:8]), ACT.Copy)
+        terms = [obs_pair[:].rearrange("p v t -> p (v t)")] + [pair[:, d, :] for d in range(D)]
+        turned = psum.tile([P, P], F32, name="turned", tag="sum")
+        for n, term in enumerate(terms):
+            nc.tensor.matmul(turned[:], term, ident[:], start=(n == 0), stop=(n == D), is_transpose=True)
+        turned_sb = keep.tile([P, P], F32, name="turned_sb", align_bytes=64)
+        nc.scalar.activation(turned_sb[:], turned[:], ACT.Copy, scale=mean_factor[:])
+        back = psum.tile([P, P], F32, name="back", tag="sum")
+        nc.tensor.transpose(back[:], turned_sb[:], ident[:])
 
-        centres = []
-        for h in range(2):
-            members = [pairs[h][:, d, :] for d in range(D)]
-            observed = [obs_pair[h][:].rearrange("p v t -> p (v t)")]
-            terms = observed + members
-            turned = psum.tile([P, P], F32, name="turned%d" % h, tag="sum%d" % h)
-            for n, term in enumerate(terms):
-                nc.tensor.matmul(turned[:], term, ident[:], start=(n == 0), stop=(n == D), is_transpose=True)
-            turned_sb = keep.tile([P, P], F32, name="turned_sb%d" % h, tag="turned_sb%d" % h, align_bytes=64)
-            nc.scalar.activation(turned_sb[:], turned[:], ACT.Copy, scale=mean_factor[:] if h == 0 else MEAN_FACTOR)
-            if h == 0:
-                anomalies(3, D // 2, D, -GAIN)
-            back = psum.tile([P, P], F32, name="back%d" % h, tag="sum%d" % h)
-            nc.tensor.transpose(back[:], turned_sb[:], ident[:])
-            centres.append(back)
-        ens_late = turns.tile([P, CH], F32, name="ens_late", align_bytes=64, offset=0)
-        nc.vector.tensor_copy(ens_late[:], ens_sb[1][:].indirect(offsets[:, 24:32]))
-        ens_g = [ens_early[:, :, CH * c : CH * (c + 1)] for c in range(3)] + [(ens_early[:, 0, S - CH : S], ens_late[:])]
-        cen_last = keep.tile([P, VC, 4], F32, name="cen_last", align_bytes=64)
-        nc.vector.scalar_tensor_tensor(
-            cen_last[:],
-            sums[:].rearrange("p t v -> p v t"),
-            -(1.0 - GAIN) / D,
-            obs_vt[:, 2 * VC : 3 * VC, :],
-            ALU.mult,
-            ALU.add,
-        )
-        cen = [
-            centres[0][:, 0:W],
-            centres[0][:, W : 2 * W],
-            cen_last[:].rearrange("p v t -> p (v t)"),
-            centres[1][:, W : 2 * W],
-        ]
+        ens_g = keep.tile([P, 2, S], F32, name="ens_g", tag="mean_factor", align_bytes=64)
+        for a, lo, hi in ((1, 0, 2), (0, 1, 4), (1, 2, 4)):
+            nc.scalar.activation(ens_g[:, a, CH * lo : CH * hi], ens_sb[a][:].indirect(offsets[:, 8 * lo : 8 * hi]), ACT.Copy)
 
-        w2_g = keep.tile([P, N, 4], BF16, name="w2_g", tag="mean_factor", align_bytes=64)
-        nc.scalar.copy(
-            w2_g[:].rearrange("p (c i) j -> p c j i", i=4),
-            w2_raw[:].rearrange("p j (c i) -> p c j i", i=4),
-        )
+        sums, cen = {}, {1: back[:, 0:W], 2: back[:, W : 2 * W]}
+
+        def reduce(c):
+            sums[c] = keep.tile([P, 4, VC], F32, name="sums%d" % c, align_bytes=64)
+            nc.vector.tensor_reduce(sums[c][:], y[c][:].rearrange("p t (v d) -> p t v d", d=D), AX.X, ALU.add)
+
+        def centre(c):
+            made = keep.tile([P, VC, 4], F32, name="cen%d" % c, align_bytes=64)
+            nc.vector.scalar_tensor_tensor(
+                made[:],
+                sums[c][:].rearrange("p t v -> p v t"),
+                -(1.0 - GAIN) / D,
+                obs_vt[:, VC * c : VC * (c + 1), :],
+                ALU.mult,
+                ALU.add,
+            )
+            cen[c] = made[:].rearrange("p v t -> p (v t)")
+
+        w2_g = keep.tile([P, N, 4], BF16, name="w2_g", align_bytes=64)
         w2_c = keep.tile([P, N], U32, name="w2_c", align_bytes=64)
         w2_s = keep.tile([P, N], U8, name="w2_s", align_bytes=64)
 
@@ -178,22 +162,29 @@ def tile_picked_yenkf_third_p_kernel(tc, x_words, x_scales, w1, obs, w2, ens, of
 
         def combine(c):
             rr[c] = keep.tile([P, D, W], BF16, name="rr%d" % c, align_bytes=64)
-            engine = nc.gpsimd if c == 2 else nc.vector
-            engine.tensor_tensor(rr[c][:], anom[c], cen[c].unsqueeze(1).to_broadcast([P, D, W]), ALU.add)
+            if c == 0:
+                nc.gpsimd.tensor_tensor(rr[c][:, 0:SHARED, :], anom[c], cen[c].unsqueeze(1).to_broadcast([P, SHARED, W]), ALU.add)
+                for d in range(SHARED, D):
+                    nc.vector.scalar_tensor_tensor(
+                        rr[c][:, d, :].rearrange("p (v t) -> p v t", t=4),
+                        y[c][:].rearrange("p t (v d) -> p d v t", d=D)[:, d, :, :],
+                        -GAIN,
+                        cen[c].rearrange("p (v t) -> p v t", t=4),
+                        ALU.mult,
+                        ALU.add,
+                    )
+            else:
+                engine = nc.gpsimd if c == 3 else nc.vector
+                engine.tensor_tensor(rr[c][:], anom[c], cen[c].unsqueeze(1).to_broadcast([P, D, W]), ALU.add)
 
         def product(c):
-            r_c = keep.tile([P, CH], U32, name="r_c%d" % c, tag="pair0" if c == 2 else "r_c%d" % c, align_bytes=64)
+            r_c = keep.tile([P, CH], U32, name="r_c%d" % c, align_bytes=64)
             r_s = keep.tile([P, CH], U8, name="r_s%d" % c, align_bytes=64)
             nc.vector.quantize_mx(out=r_c[:].bitcast(X4), scales=r_s[:], in_=rr[c][:].rearrange("p d w -> p (d w)"))
-            if c == 3:
-                z[c] = [psum.tile([P, CH], F32, name="z3_%d" % a, tag=("bank3", "warm")[a])[:] for a in range(2)]
-                halves = z[c]
-            else:
-                z[c] = psum.tile([P, 2, CH], F32, name="z%d" % c, tag="bank%d" % c)
-                halves = [z[c][:, a, :] for a in range(2)]
+            z[c] = psum.tile([P, 2, CH], F32, name="z%d" % c, tag="bank%d" % c)
             for a in range(2):
                 nc.tensor.matmul_mx(
-                    out=halves[a],
+                    out=z[c][:, a, :],
                     lhsT=w2_c[:, P * a : P * (a + 1)].bitcast(X4),
                     lhsT_scale=w2_s[:, P * a : P * (a + 1)],
                     rhs=r_c[:].bitcast(X4),
@@ -204,31 +195,38 @@ def tile_picked_yenkf_third_p_kernel(tc, x_words, x_scales, w1, obs, w2, ens, of
 
         def finish(c):
             res = keep.tile([P, 2, CH], F32, name="res%d" % c, align_bytes=64)
-            if c == 3:
-                for a in range(2):
+            if c == 0:
+                for a, picked in enumerate((ens_first[:], ens_g[:, 1, 0:CH])):
                     nc.vector.tensor_tensor(
                         res[:, a, :].rearrange("p (v d) -> p v d", d=D),
-                        z[c][a].rearrange("p (d v) -> p v d", d=D),
-                        ens_g[c][a].rearrange("p (v d) -> p v d", d=D),
+                        z[c][:, a, :].rearrange("p (d v) -> p v d", d=D),
+                        picked.rearrange("p (v d) -> p v d", d=D),
                         ALU.add,
                     )
             else:
                 nc.vector.tensor_tensor(
                     res[:].rearrange("p a (v d) -> p a v d", d=D),
                     z[c][:].rearrange("p a (d v) -> p a v d", d=D),
-                    ens_g[c].rearrange("p a (v d) -> p a v d", d=D),
+                    ens_g[:, :, CH * c : CH * (c + 1)].rearrange("p a (v d) -> p a v d", d=D),
                     ALU.add,
                 )
             nc.sync.dma_start(outv[:, :, CH * c : CH * (c + 1)], res[:])
 
-        combine(2)
-        combine(0)
-        combine(1)
+        nc.vector.tensor_copy(
+            w2_g[:].rearrange("p (c i) j -> p c j i", i=4),
+            w2_raw[:].rearrange("p j (c i) -> p c j i", i=4),
+        )
+        reduce(0)
         nc.vector.quantize_mx(out=w2_c[:].bitcast(X4), scales=w2_s[:], in_=w2_g[:].rearrange("p c j -> p (c j)"))
-        for c in range(3):
-            product(c)
+        centre(0)
+        combine(0)
+        reduce(3)
+        product(0)
+        centre(3)
         combine(3)
-        finish(0)
-        product(3)
-        for c in (1, 2, 3):
+        combine(1)
+        combine(2)
+        for c in (1, 3, 2):
+            product(c)
+        for c in (0, 1, 3, 2):
             finish(c)

@@ -20,7 +20,9 @@ NCH = S // CH
 VC = CH // D
 GAIN = 0.3
 W1_PIECES = ((0, 64), (64, 128))
-SHARED = 5
+FIRST, LAST = 3, 2
+FIRST_SHARE = 5
+PAIR_SHARE = 3
 MEAN_FACTOR = (1.0 - GAIN) / (GAIN * D)
 
 
@@ -77,36 +79,25 @@ def tile_picked_yenkf_third_p_kernel(tc, x_words, x_scales, w1, obs, w2, ens, of
 
         W = 4 * VC
         pair = keep.tile([P, D, 2 * W], F32, name="pair", align_bytes=64)
-        anom_last = keep.tile([P, D, W], F32, name="anom_last", align_bytes=64)
-        anom_first = keep.tile([P, SHARED, W], F32, name="anom_first", align_bytes=64)
-        anom = {0: anom_first[:], 1: pair[:, :, 0:W], 2: pair[:, :, W : 2 * W], 3: anom_last[:]}
+        anom_first = keep.tile([P, FIRST_SHARE, W], F32, name="anom_first", align_bytes=64)
+        anom_last = keep.tile([P, 2, CH, 2], F32, name="anom_last", align_bytes=64)
         obs_vt = obs_sb[:].rearrange("p t v -> p v t")
         obs_pair = keep.tile([P, 2 * VC, 4], F32, name="obs_pair", align_bytes=64)
-        nc.gpsimd.tensor_scalar(obs_pair[:], obs_vt[:, VC : 3 * VC, :], 1.0 / MEAN_FACTOR, 0.0, ALU.mult, ALU.add)
+        nc.gpsimd.tensor_scalar(obs_pair[:], obs_vt[:, 0 : 2 * VC, :], 1.0 / MEAN_FACTOR, 0.0, ALU.mult, ALU.add)
 
-        mean_factor = keep.tile([P, 1], F32, name="mean_factor", tag="mean_factor", align_bytes=64)
-        nc.gpsimd.memset(mean_factor[:], 1.0)
-        nc.gpsimd.tensor_scalar(mean_factor[:], mean_factor[:], MEAN_FACTOR, 0.0, ALU.mult, ALU.add)
-
-        def anomalies(c, lo, hi):
-            nc.scalar.activation(
-                anom[c][:, lo:hi, :].rearrange("p d (v t) -> p d v t", t=4),
-                y[c][:].rearrange("p t (v d) -> p d v t", d=D)[:, lo:hi, :, :],
-                ACT.Copy,
-                scale=-GAIN,
-            )
+        ens_edge = keep.tile([P, 2, 2 * CH], F32, name="ens_edge", align_bytes=64)
+        mean_factor = ens_edge[:, 1, 0:1]
+        nc.gpsimd.memset(mean_factor, 1.0)
+        nc.gpsimd.tensor_scalar(mean_factor, mean_factor, MEAN_FACTOR, 0.0, ALU.mult, ALU.add)
 
         xw = keep.tile([P, S], U32, name="xw", tag="w1_g1", align_bytes=64)
-        y = []
-        for c in range(NCH):
-            if c < 3:
-                last = c + 1 if c < 2 else NCH
-                nc.vector.tensor_copy(xw[:, CH * c : CH * last], xw_all[:].bitcast(U32).indirect(offsets[:, 8 * c : 8 * last]))
-            yc = psum.tile([P, 4, CH], F32, name="y%d" % c, tag="bank%d" % c)
-            y.append(yc)
+        for lo, hi in ((FIRST, FIRST + 1), (0, 1), (1, LAST + 1)):
+            nc.vector.tensor_copy(xw[:, CH * lo : CH * hi], xw_all[:].bitcast(U32).indirect(offsets[:, 8 * lo : 8 * hi]))
+
+        def first_product(c, tiles):
             for t in range(4):
                 nc.tensor.matmul_mx(
-                    out=yc[:, t, :],
+                    out=tiles[t],
                     lhsT=w1_c[:, P * t : P * (t + 1)].bitcast(X4),
                     lhsT_scale=w1_s[:, P * t : P * (t + 1)],
                     rhs=xw[:, CH * c : CH * (c + 1)].bitcast(X4),
@@ -114,119 +105,148 @@ def tile_picked_yenkf_third_p_kernel(tc, x_words, x_scales, w1, obs, w2, ens, of
                     start=True,
                     stop=True,
                 )
-            if c == 2:
-                anomalies(c, 0, D // 2)
-                anomalies(c, D // 2, D)
-            else:
-                anomalies(c, 0, D if c > 0 else SHARED)
 
-        ens_first = keep.tile([P, CH], F32, name="ens_first", align_bytes=64)
-        nc.scalar.activation(ens_first[:], ens_sb[0][:].indirect(offsets[:, 0:8]), ACT.Copy)
-        terms = [obs_pair[:].rearrange("p v t -> p (v t)")] + [pair[:, d, :] for d in range(D)]
-        turned = psum.tile([P, P], F32, name="turned", tag="sum")
-        for n, term in enumerate(terms):
-            nc.tensor.matmul(turned[:], term, ident[:], start=(n == 0), stop=(n == D), is_transpose=True)
-        turned_sb = keep.tile([P, P], F32, name="turned_sb", align_bytes=64)
-        nc.scalar.activation(turned_sb[:], turned[:], ACT.Copy, scale=mean_factor[:])
-        back = psum.tile([P, P], F32, name="back", tag="sum")
-        nc.tensor.transpose(back[:], turned_sb[:], ident[:])
+        def by_member(bank):
+            return bank[:].rearrange("p t (v d) -> p d v t", d=D)
 
-        ens_g = keep.tile([P, 2, S], F32, name="ens_g", tag="mean_factor", align_bytes=64)
-        for a, lo, hi in ((1, 0, 2), (0, 1, 4), (1, 2, 4)):
-            nc.scalar.activation(ens_g[:, a, CH * lo : CH * hi], ens_sb[a][:].indirect(offsets[:, 8 * lo : 8 * hi]), ACT.Copy)
+        def anomalies(dst, bank, lo, hi):
+            nc.scalar.activation(dst, by_member(bank)[:, lo:hi, :, :], ACT.Copy, scale=-GAIN)
 
-        sums, cen = {}, {1: back[:, 0:W], 2: back[:, W : 2 * W]}
+        def reduce(dst, bank):
+            nc.vector.tensor_reduce(dst, bank[:].rearrange("p t (v d) -> p t v d", d=D), AX.X, ALU.add)
 
-        def reduce(c):
-            sums[c] = keep.tile([P, 4, VC], F32, name="sums%d" % c, align_bytes=64)
-            nc.vector.tensor_reduce(sums[c][:], y[c][:].rearrange("p t (v d) -> p t v d", d=D), AX.X, ALU.add)
-
-        def centre(c):
+        def centre(c, sums):
             made = keep.tile([P, VC, 4], F32, name="cen%d" % c, align_bytes=64)
             nc.vector.scalar_tensor_tensor(
                 made[:],
-                sums[c][:].rearrange("p t v -> p v t"),
+                sums[:].rearrange("p t v -> p v t"),
                 -(1.0 - GAIN) / D,
                 obs_vt[:, VC * c : VC * (c + 1), :],
                 ALU.mult,
                 ALU.add,
             )
-            cen[c] = made[:].rearrange("p v t -> p (v t)")
+            return made
+
+        y_first = psum.tile([P, 4, CH], F32, name="y_first", tag="first")
+        first_product(FIRST, [y_first[:, t, :] for t in range(4)])
+        anomalies(anom_first[:].rearrange("p d (v t) -> p d v t", t=4), y_first, 0, FIRST_SHARE)
+        for c in range(2):
+            y_pair = psum.tile([P, 4, CH], F32, name="y_pair%d" % c, tag="pair%d" % c)
+            first_product(c, [y_pair[:, t, :] for t in range(4)])
+            for lo, hi in ((0, D),) if c == 0 else ((0, D // 2), (D // 2, D)):
+                anomalies(pair[:, lo:hi, W * c : W * (c + 1)].rearrange("p d (v t) -> p d v t", t=4), y_pair, lo, hi)
+        y_last = [psum.tile([P, 2, CH], F32, name="y_last%d" % u, tag="last%d" % u) for u in range(2)]
+        first_product(LAST, [y_last[t // 2][:, t % 2, :] for t in range(4)])
 
         w2_g = keep.tile([P, N, 4], BF16, name="w2_g", align_bytes=64)
         w2_c = keep.tile([P, N], U32, name="w2_c", align_bytes=64)
         w2_s = keep.tile([P, N], U8, name="w2_s", align_bytes=64)
-
-        outv = out.rearrange("(a p) j -> p a j", p=P)
-        rr, z = {}, {}
-
-        def combine(c):
-            rr[c] = keep.tile([P, D, W], BF16, name="rr%d" % c, align_bytes=64)
-            if c == 0:
-                nc.gpsimd.tensor_tensor(rr[c][:, 0:SHARED, :], anom[c], cen[c].unsqueeze(1).to_broadcast([P, SHARED, W]), ALU.add)
-                for d in range(SHARED, D):
-                    nc.vector.scalar_tensor_tensor(
-                        rr[c][:, d, :].rearrange("p (v t) -> p v t", t=4),
-                        y[c][:].rearrange("p t (v d) -> p d v t", d=D)[:, d, :, :],
-                        -GAIN,
-                        cen[c].rearrange("p (v t) -> p v t", t=4),
-                        ALU.mult,
-                        ALU.add,
-                    )
-            else:
-                engine = nc.gpsimd if c == 3 else nc.vector
-                engine.tensor_tensor(rr[c][:], anom[c], cen[c].unsqueeze(1).to_broadcast([P, D, W]), ALU.add)
-
-        def product(c):
-            r_c = keep.tile([P, CH], U32, name="r_c%d" % c, align_bytes=64)
-            r_s = keep.tile([P, CH], U8, name="r_s%d" % c, align_bytes=64)
-            nc.vector.quantize_mx(out=r_c[:].bitcast(X4), scales=r_s[:], in_=rr[c][:].rearrange("p d w -> p (d w)"))
-            z[c] = psum.tile([P, 2, CH], F32, name="z%d" % c, tag="bank%d" % c)
-            for a in range(2):
-                nc.tensor.matmul_mx(
-                    out=z[c][:, a, :],
-                    lhsT=w2_c[:, P * a : P * (a + 1)].bitcast(X4),
-                    lhsT_scale=w2_s[:, P * a : P * (a + 1)],
-                    rhs=r_c[:].bitcast(X4),
-                    rhs_scale=r_s[:],
-                    start=True,
-                    stop=True,
-                )
-
-        def finish(c):
-            res = keep.tile([P, 2, CH], F32, name="res%d" % c, align_bytes=64)
-            if c == 0:
-                for a, picked in enumerate((ens_first[:], ens_g[:, 1, 0:CH])):
-                    nc.vector.tensor_tensor(
-                        res[:, a, :].rearrange("p (v d) -> p v d", d=D),
-                        z[c][:, a, :].rearrange("p (d v) -> p v d", d=D),
-                        picked.rearrange("p (v d) -> p v d", d=D),
-                        ALU.add,
-                    )
-            else:
-                nc.vector.tensor_tensor(
-                    res[:].rearrange("p a (v d) -> p a v d", d=D),
-                    z[c][:].rearrange("p a (d v) -> p a v d", d=D),
-                    ens_g[:, :, CH * c : CH * (c + 1)].rearrange("p a (v d) -> p a v d", d=D),
-                    ALU.add,
-                )
-            nc.sync.dma_start(outv[:, :, CH * c : CH * (c + 1)], res[:])
-
         nc.vector.tensor_copy(
             w2_g[:].rearrange("p (c i) j -> p c j i", i=4),
             w2_raw[:].rearrange("p j (c i) -> p c j i", i=4),
         )
-        reduce(0)
+        sums_first = keep.tile([P, 4, VC], F32, name="sums_first", align_bytes=64)
+        reduce(sums_first[:], y_first)
         nc.vector.quantize_mx(out=w2_c[:].bitcast(X4), scales=w2_s[:], in_=w2_g[:].rearrange("p c j -> p (c j)"))
-        centre(0)
-        combine(0)
-        reduce(3)
-        product(0)
-        centre(3)
-        combine(3)
-        combine(1)
-        combine(2)
-        for c in (1, 3, 2):
-            product(c)
-        for c in (0, 1, 3, 2):
-            finish(c)
+        cen_first = centre(FIRST, sums_first)
+        rr_first = keep.tile([P, D, W], BF16, name="rr_first", align_bytes=64)
+        nc.gpsimd.tensor_tensor(
+            rr_first[:, 0:FIRST_SHARE, :],
+            anom_first[:],
+            cen_first[:].rearrange("p v t -> p (v t)").unsqueeze(1).to_broadcast([P, FIRST_SHARE, W]),
+            ALU.add,
+        )
+
+        sums_last = keep.tile([P, 4, VC], F32, name="sums_last", align_bytes=64)
+        last_halves = [anom_last[:, u, :, :].rearrange("p (d v) t -> p d v t", d=D) for u in range(2)]
+        anomalies(last_halves[0], y_last[0], 0, D)
+        for u in (1, 0):
+            reduce(sums_last[:, 2 * u : 2 * u + 2, :], y_last[u])
+        anomalies(last_halves[1], y_last[1], 0, D)
+
+        def pick(dst, a, lo):
+            nc.scalar.activation(dst, ens_sb[a][:].indirect(offsets[:, 8 * lo : 8 * (lo + 2)]), ACT.Copy)
+
+        pick(ens_edge[:, 0, :], 0, 2)
+        terms = [obs_pair[:].rearrange("p v t -> p (v t)")] + [pair[:, d, :] for d in range(D)]
+        turned = psum.tile([P, P], F32, name="turned", tag="sum")
+        for n, term in enumerate(terms):
+            nc.tensor.matmul(turned[:], term, ident[:], start=(n == 0), stop=(n == D), is_transpose=True)
+        turned_sb = keep.tile([P, P], F32, name="turned_sb", tag="turned_sb", align_bytes=64)
+        nc.scalar.activation(turned_sb[:], turned[:], ACT.Copy, scale=mean_factor)
+        cen_pair = psum.tile([P, P], F32, name="cen_pair", tag="sum")
+        nc.tensor.transpose(cen_pair[:], turned_sb[:], ident[:])
+        cen_again = psum.tile([P, P], F32, name="cen_again", tag="again")
+        nc.tensor.transpose(cen_again[:], turned_sb[:], ident[:])
+        cen_sb = keep.tile([P, W], F32, name="cen_sb", align_bytes=64)
+        nc.scalar.copy(cen_sb[:], cen_again[:, W : 2 * W])
+
+        pick(ens_edge[:, 1, :], 1, 2)
+        ens_pair = keep.tile([P, 2, 2 * CH], F32, name="ens_pair", tag="turned_sb", align_bytes=64)
+        for a in range(2):
+            pick(ens_pair[:, a, :], a, 0)
+
+        def quantise(name, rr, width):
+            codes = keep.tile([P, width], U32, name="codes_" + name, align_bytes=64)
+            scales = keep.tile([P, width], U8, name="scales_" + name, align_bytes=64)
+            nc.vector.quantize_mx(out=codes[:].bitcast(X4), scales=scales[:], in_=rr[:].rearrange("p d w -> p (d w)"))
+            return codes, scales
+
+        def second_product(halves, codes, scales):
+            for a in range(2):
+                nc.tensor.matmul_mx(
+                    out=halves[a],
+                    lhsT=w2_c[:, P * a : P * (a + 1)].bitcast(X4),
+                    lhsT_scale=w2_s[:, P * a : P * (a + 1)],
+                    rhs=codes[:].bitcast(X4),
+                    rhs_scale=scales[:],
+                    start=True,
+                    stop=True,
+                )
+
+        outv = out.rearrange("(a p) j -> p a j", p=P)
+
+        def finish(c, z):
+            picked = ens_pair if c < 2 else ens_edge
+            res = keep.tile([P, 2, CH], F32, name="res%d" % c, tag="rr_last" if c == FIRST else "res%d" % c, align_bytes=64)
+            nc.vector.tensor_tensor(
+                res[:].rearrange("p a (v d) -> p a v d", d=D),
+                z[:].rearrange("p a (d v) -> p a v d", d=D),
+                picked[:, :, CH * (c % 2) : CH * (c % 2 + 1)].rearrange("p a (v d) -> p a v d", d=D),
+                ALU.add,
+            )
+            nc.sync.dma_start(outv[:, :, CH * c : CH * (c + 1)], res[:])
+
+        for d in range(FIRST_SHARE, D):
+            nc.vector.scalar_tensor_tensor(
+                rr_first[:, d, :].rearrange("p (v t) -> p v t", t=4),
+                by_member(y_first)[:, d, :, :],
+                -GAIN,
+                cen_first[:],
+                ALU.mult,
+                ALU.add,
+            )
+        cen_last = centre(LAST, sums_last)
+        z_first = psum.tile([P, 2, CH], F32, name="z_first", tag="again")
+        second_product([z_first[:, a, :] for a in range(2)], *quantise("first", rr_first, CH))
+        rr_last = keep.tile([P, D, W], BF16, name="rr_last", tag="rr_last", align_bytes=64)
+        nc.gpsimd.tensor_tensor(
+            rr_last[:].rearrange("p d w -> p (d w)"),
+            anom_last[:].rearrange("p u c t -> p c u t"),
+            cen_last[:].rearrange("p v t -> p (v t)").unsqueeze(1).to_broadcast([P, D, W]),
+            ALU.add,
+        )
+        rr_pair = [keep.tile([P, D, W], BF16, name="rr_pair%d" % c, align_bytes=64) for c in range(2)]
+        for engine, c, lo, hi, cen in (
+            (nc.vector, 0, 0, D, cen_pair[:, 0:W]),
+            (nc.gpsimd, 1, 0, PAIR_SHARE, cen_sb[:]),
+            (nc.vector, 1, PAIR_SHARE, D, cen_pair[:, W : 2 * W]),
+        ):
+            engine.tensor_tensor(rr_pair[c][:, lo:hi, :], pair[:, lo:hi, W * c : W * (c + 1)], cen.unsqueeze(1).to_broadcast([P, hi - lo, W]), ALU.add)
+
+        z = {FIRST: z_first}
+        for c, rr, bank in ((0, rr_pair[0], "pair0"), (LAST, rr_last, "last0"), (1, rr_pair[1], "pair1")):
+            z[c] = psum.tile([P, 2, CH], F32, name="z%d" % c, tag=bank)
+            second_product([z[c][:, a, :] for a in range(2)], *quantise(bank, rr, CH))
+        for c in (FIRST, 0, LAST, 1):
+            finish(c, z[c])

@@ -22,7 +22,6 @@ GAIN = 0.3
 W1_PIECES = ((0, 64), (64, 128))
 FIRST, LAST = 3, 2
 FIRST_SHARE = 5
-PAIR_SHARE = 3
 MEAN_FACTOR = (1.0 - GAIN) / (GAIN * D)
 
 
@@ -164,27 +163,24 @@ def tile_picked_yenkf_third_p_kernel(tc, x_words, x_scales, w1, obs, w2, ens, of
             reduce(sums_last[:, 2 * u : 2 * u + 2, :], y_last[u])
         anomalies(last_halves[1], y_last[1], 0, D)
 
-        def pick(dst, a, lo):
-            nc.scalar.activation(dst, ens_sb[a][:].indirect(offsets[:, 8 * lo : 8 * (lo + 2)]), ACT.Copy)
+        def pick(dst, a, lo, hi):
+            nc.scalar.activation(dst, ens_sb[a][:].indirect(offsets[:, 8 * lo : 8 * hi]), ACT.Copy)
 
-        pick(ens_edge[:, 0, :], 0, 2)
+        pick(ens_edge[:, 0, CH : 2 * CH], 0, FIRST, FIRST + 1)
         terms = [obs_pair[:].rearrange("p v t -> p (v t)")] + [pair[:, d, :] for d in range(D)]
         turned = psum.tile([P, P], F32, name="turned", tag="sum")
         for n, term in enumerate(terms):
             nc.tensor.matmul(turned[:], term, ident[:], start=(n == 0), stop=(n == D), is_transpose=True)
         turned_sb = keep.tile([P, P], F32, name="turned_sb", tag="turned_sb", align_bytes=64)
         nc.scalar.activation(turned_sb[:], turned[:], ACT.Copy, scale=mean_factor)
-        cen_pair = psum.tile([P, P], F32, name="cen_pair", tag="sum")
+        cen_pair = psum.tile([P, P], F32, name="cen_pair", tag="back")
         nc.tensor.transpose(cen_pair[:], turned_sb[:], ident[:])
-        cen_again = psum.tile([P, P], F32, name="cen_again", tag="again")
-        nc.tensor.transpose(cen_again[:], turned_sb[:], ident[:])
-        cen_sb = keep.tile([P, W], F32, name="cen_sb", align_bytes=64)
-        nc.scalar.copy(cen_sb[:], cen_again[:, W : 2 * W])
 
-        pick(ens_edge[:, 1, :], 1, 2)
+        pick(ens_edge[:, 1, :], 1, 2, 4)
         ens_pair = keep.tile([P, 2, 2 * CH], F32, name="ens_pair", tag="turned_sb", align_bytes=64)
-        for a in range(2):
-            pick(ens_pair[:, a, :], a, 0)
+        for c in range(2):
+            for a in range(2):
+                pick(ens_pair[:, a, CH * c : CH * (c + 1)], a, c, c + 1)
 
         def quantise(name, rr, width):
             codes = keep.tile([P, width], U32, name="codes_" + name, align_bytes=64)
@@ -226,8 +222,9 @@ def tile_picked_yenkf_third_p_kernel(tc, x_words, x_scales, w1, obs, w2, ens, of
                 ALU.mult,
                 ALU.add,
             )
+        nc.vector.tensor_copy(ens_edge[:, 0, 0:CH], ens_sb[0][:].indirect(offsets[:, 8 * LAST : 8 * (LAST + 1)]))
         cen_last = centre(LAST, sums_last)
-        z_first = psum.tile([P, 2, CH], F32, name="z_first", tag="again")
+        z_first = psum.tile([P, 2, CH], F32, name="z_first", tag="sum")
         second_product([z_first[:, a, :] for a in range(2)], *quantise("first", rr_first, CH))
         rr_last = keep.tile([P, D, W], BF16, name="rr_last", tag="rr_last", align_bytes=64)
         nc.gpsimd.tensor_tensor(
@@ -237,16 +234,13 @@ def tile_picked_yenkf_third_p_kernel(tc, x_words, x_scales, w1, obs, w2, ens, of
             ALU.add,
         )
         rr_pair = [keep.tile([P, D, W], BF16, name="rr_pair%d" % c, align_bytes=64) for c in range(2)]
-        for engine, c, lo, hi, cen in (
-            (nc.vector, 0, 0, D, cen_pair[:, 0:W]),
-            (nc.gpsimd, 1, 0, PAIR_SHARE, cen_sb[:]),
-            (nc.vector, 1, PAIR_SHARE, D, cen_pair[:, W : 2 * W]),
-        ):
-            engine.tensor_tensor(rr_pair[c][:, lo:hi, :], pair[:, lo:hi, W * c : W * (c + 1)], cen.unsqueeze(1).to_broadcast([P, hi - lo, W]), ALU.add)
+        for c in range(2):
+            cols = slice(W * c, W * (c + 1))
+            nc.vector.tensor_tensor(rr_pair[c][:], pair[:, :, cols], cen_pair[:, cols].unsqueeze(1).to_broadcast([P, D, W]), ALU.add)
 
         z = {FIRST: z_first}
-        for c, rr, bank in ((0, rr_pair[0], "pair0"), (LAST, rr_last, "last0"), (1, rr_pair[1], "pair1")):
+        for c, rr, bank in ((LAST, rr_last, "last0"), (0, rr_pair[0], "pair0"), (1, rr_pair[1], "pair1")):
             z[c] = psum.tile([P, 2, CH], F32, name="z%d" % c, tag=bank)
             second_product([z[c][:, a, :] for a in range(2)], *quantise(bank, rr, CH))
-        for c in (FIRST, 0, LAST, 1):
+        for c in (FIRST, LAST, 0, 1):
             finish(c, z[c])

@@ -84,10 +84,10 @@ def tile_picked_yenkf_third_p_kernel(tc, x_words, x_scales, w1, obs, w2, ens, of
         obs_pair = keep.tile([P, 2 * VC, 4], F32, name="obs_pair", align_bytes=64)
         nc.gpsimd.tensor_scalar(obs_pair[:], obs_vt[:, 0 : 2 * VC, :], 1.0 / MEAN_FACTOR, 0.0, ALU.mult, ALU.add)
 
-        ens_edge = keep.tile([P, 2, 2 * CH], F32, name="ens_edge", align_bytes=64)
-        mean_factor = ens_edge[:, 1, 0:1]
-        nc.gpsimd.memset(mean_factor, 1.0)
-        nc.gpsimd.tensor_scalar(mean_factor, mean_factor, MEAN_FACTOR, 0.0, ALU.mult, ALU.add)
+        ens_first = keep.tile([P, 2, CH], F32, name="ens_first", align_bytes=64)
+        mean_factor = keep.tile([P, 1], F32, name="mean_factor", tag="mean_factor", align_bytes=64)
+        nc.gpsimd.memset(mean_factor[:], 1.0)
+        nc.gpsimd.tensor_scalar(mean_factor[:], mean_factor[:], MEAN_FACTOR, 0.0, ALU.mult, ALU.add)
 
         xw = keep.tile([P, S], U32, name="xw", tag="w1_g1", align_bytes=64)
         for lo, hi in ((FIRST, FIRST + 1), (0, 1), (1, LAST + 1)):
@@ -166,21 +166,21 @@ def tile_picked_yenkf_third_p_kernel(tc, x_words, x_scales, w1, obs, w2, ens, of
         def pick(dst, a, lo, hi):
             nc.scalar.activation(dst, ens_sb[a][:].indirect(offsets[:, 8 * lo : 8 * hi]), ACT.Copy)
 
-        pick(ens_edge[:, 0, CH : 2 * CH], 0, FIRST, FIRST + 1)
+        pick(ens_first[:, 0, :], 0, FIRST, FIRST + 1)
         terms = [obs_pair[:].rearrange("p v t -> p (v t)")] + [pair[:, d, :] for d in range(D)]
         turned = psum.tile([P, P], F32, name="turned", tag="sum")
         for n, term in enumerate(terms):
             nc.tensor.matmul(turned[:], term, ident[:], start=(n == 0), stop=(n == D), is_transpose=True)
-        turned_sb = keep.tile([P, P], F32, name="turned_sb", tag="turned_sb", align_bytes=64)
-        nc.scalar.activation(turned_sb[:], turned[:], ACT.Copy, scale=mean_factor)
+        turned_sb = keep.tile([P, P], F32, name="turned_sb", align_bytes=64)
+        nc.scalar.activation(turned_sb[:], turned[:], ACT.Copy, scale=mean_factor[:])
         cen_pair = psum.tile([P, P], F32, name="cen_pair", tag="back")
         nc.tensor.transpose(cen_pair[:], turned_sb[:], ident[:])
 
-        pick(ens_edge[:, 1, :], 1, 2, 4)
-        ens_pair = keep.tile([P, 2, 2 * CH], F32, name="ens_pair", tag="turned_sb", align_bytes=64)
-        for c in range(2):
+        pick(ens_first[:, 1, :], 1, FIRST, FIRST + 1)
+        ens_rest = keep.tile([P, 2, 3 * CH], F32, name="ens_rest", tag="mean_factor", align_bytes=64)
+        for lo, hi in ((LAST, LAST + 1), (0, 2)):
             for a in range(2):
-                pick(ens_pair[:, a, CH * c : CH * (c + 1)], a, c, c + 1)
+                pick(ens_rest[:, a, CH * lo : CH * hi], a, lo, hi)
 
         def quantise(name, rr, width):
             codes = keep.tile([P, width], U32, name="codes_" + name, align_bytes=64)
@@ -188,30 +188,38 @@ def tile_picked_yenkf_third_p_kernel(tc, x_words, x_scales, w1, obs, w2, ens, of
             nc.vector.quantize_mx(out=codes[:].bitcast(X4), scales=scales[:], in_=rr[:].rearrange("p d w -> p (d w)"))
             return codes, scales
 
-        def second_product(halves, codes, scales):
-            for a in range(2):
-                nc.tensor.matmul_mx(
-                    out=halves[a],
-                    lhsT=w2_c[:, P * a : P * (a + 1)].bitcast(X4),
-                    lhsT_scale=w2_s[:, P * a : P * (a + 1)],
-                    rhs=codes[:].bitcast(X4),
-                    rhs_scale=scales[:],
-                    start=True,
-                    stop=True,
-                )
+        def second_product(dst, a, codes, scales):
+            nc.tensor.matmul_mx(
+                out=dst,
+                lhsT=w2_c[:, P * a : P * (a + 1)].bitcast(X4),
+                lhsT_scale=w2_s[:, P * a : P * (a + 1)],
+                rhs=codes[:].bitcast(X4),
+                rhs_scale=scales[:],
+                start=True,
+                stop=True,
+            )
 
         outv = out.rearrange("(a p) j -> p a j", p=P)
 
-        def finish(c, z):
-            picked = ens_pair if c < 2 else ens_edge
-            res = keep.tile([P, 2, CH], F32, name="res%d" % c, tag="rr_last" if c == FIRST else "res%d" % c, align_bytes=64)
+        def finish_chunk(c, z, picked):
+            res = keep.tile([P, 2, CH], F32, name="res%d" % c, tag="rr_last" if c == FIRST else "res", align_bytes=64)
             nc.vector.tensor_tensor(
                 res[:].rearrange("p a (v d) -> p a v d", d=D),
                 z[:].rearrange("p a (d v) -> p a v d", d=D),
-                picked[:, :, CH * (c % 2) : CH * (c % 2 + 1)].rearrange("p a (v d) -> p a v d", d=D),
+                picked.rearrange("p a (v d) -> p a v d", d=D),
                 ALU.add,
             )
             nc.sync.dma_start(outv[:, :, CH * c : CH * (c + 1)], res[:])
+
+        def finish_pair(a, z):
+            res = keep.tile([P, 2, CH], F32, name="res_pair%d" % a, align_bytes=64)
+            nc.vector.tensor_tensor(
+                res[:].rearrange("p c (v d) -> p c v d", d=D),
+                z[:].rearrange("p c (d v) -> p c v d", d=D),
+                ens_rest[:, a, 0 : 2 * CH].rearrange("p (c v d) -> p c v d", c=2, d=D),
+                ALU.add,
+            )
+            nc.sync.dma_start(outv[:, a, 0 : 2 * CH], res[:].rearrange("p c j -> p (c j)"))
 
         for d in range(FIRST_SHARE, D):
             nc.vector.scalar_tensor_tensor(
@@ -222,10 +230,11 @@ def tile_picked_yenkf_third_p_kernel(tc, x_words, x_scales, w1, obs, w2, ens, of
                 ALU.mult,
                 ALU.add,
             )
-        nc.vector.tensor_copy(ens_edge[:, 0, 0:CH], ens_sb[0][:].indirect(offsets[:, 8 * LAST : 8 * (LAST + 1)]))
         cen_last = centre(LAST, sums_last)
         z_first = psum.tile([P, 2, CH], F32, name="z_first", tag="sum")
-        second_product([z_first[:, a, :] for a in range(2)], *quantise("first", rr_first, CH))
+        mx_first = quantise("first", rr_first, CH)
+        for a in range(2):
+            second_product(z_first[:, a, :], a, *mx_first)
         rr_last = keep.tile([P, D, W], BF16, name="rr_last", tag="rr_last", align_bytes=64)
         nc.gpsimd.tensor_tensor(
             rr_last[:].rearrange("p d w -> p (d w)"),
@@ -238,9 +247,16 @@ def tile_picked_yenkf_third_p_kernel(tc, x_words, x_scales, w1, obs, w2, ens, of
             cols = slice(W * c, W * (c + 1))
             nc.vector.tensor_tensor(rr_pair[c][:], pair[:, :, cols], cen_pair[:, cols].unsqueeze(1).to_broadcast([P, D, W]), ALU.add)
 
-        z = {FIRST: z_first}
-        for c, rr, bank in ((LAST, rr_last, "last0"), (0, rr_pair[0], "pair0"), (1, rr_pair[1], "pair1")):
-            z[c] = psum.tile([P, 2, CH], F32, name="z%d" % c, tag=bank)
-            second_product([z[c][:, a, :] for a in range(2)], *quantise(bank, rr, CH))
-        for c in (FIRST, LAST, 0, 1):
-            finish(c, z[c])
+        z_last = psum.tile([P, 2, CH], F32, name="z_last", tag="last0")
+        mx_last = quantise("last", rr_last, CH)
+        for a in range(2):
+            second_product(z_last[:, a, :], a, *mx_last)
+        mx_pair = [quantise("pair%d" % c, rr_pair[c], CH) for c in range(2)]
+        z_pair = [psum.tile([P, 2, CH], F32, name="z_pair%d" % a, tag="pair%d" % a) for a in range(2)]
+        for a in range(2):
+            for c in range(2):
+                second_product(z_pair[a][:, c, :], a, *mx_pair[c])
+        finish_chunk(FIRST, z_first, ens_first[:])
+        finish_chunk(LAST, z_last, ens_rest[:, :, CH * LAST : CH * (LAST + 1)])
+        for a in range(2):
+            finish_pair(a, z_pair[a])

@@ -63,13 +63,18 @@ def tile_picked_yenkf_third_p_kernel(tc, x_words, x_scales, w1, obs, w2, ens, of
         nc.vector.tensor_copy(xs[:], xs_all[:].indirect(offsets[:]))
 
         w1_g = [keep.tile([P, 2, P, 4], BF16, name="w1_g%d" % u, tag="w1_g%d" % u, align_bytes=64) for u in range(2)]
-        for raw, (lo, hi) in zip(w1_raw, W1_PIECES):
-            for u in range(2):
-                copy = nc.vector.tensor_copy if lo > 0 and u == 0 else nc.scalar.copy
-                copy(
-                    w1_g[u][:, :, lo:hi, :].rearrange("p t m j -> p m j t"),
-                    raw[:].rearrange("p j (m t) -> p m j t", t=4)[:, :, :, 2 * u : 2 * u + 2],
-                )
+        for copy, piece, u, lo, hi in (
+            (nc.scalar.copy, 0, 0, 0, 64),
+            (nc.scalar.copy, 0, 1, 0, 64),
+            (nc.vector.tensor_copy, 1, 0, 64, 128),
+            (nc.scalar.copy, 1, 1, 64, 96),
+            (nc.vector.tensor_copy, 1, 1, 96, 128),
+        ):
+            first = W1_PIECES[piece][0]
+            copy(
+                w1_g[u][:, :, lo:hi, :].rearrange("p t m j -> p m j t"),
+                w1_raw[piece][:].rearrange("p j (m t) -> p m j t", t=4)[:, lo - first : hi - first, :, 2 * u : 2 * u + 2],
+            )
         w1_c = keep.tile([P, H], U32, name="w1_c", align_bytes=64)
         w1_s = keep.tile([P, H], U8, name="w1_s", align_bytes=64)
         for u in range(2):
@@ -89,7 +94,7 @@ def tile_picked_yenkf_third_p_kernel(tc, x_words, x_scales, w1, obs, w2, ens, of
         nc.gpsimd.memset(mean_factor[:], 1.0)
         nc.gpsimd.tensor_scalar(mean_factor[:], mean_factor[:], MEAN_FACTOR, 0.0, ALU.mult, ALU.add)
 
-        xw = keep.tile([P, S], U32, name="xw", tag="w1_g1", align_bytes=64)
+        xw = keep.tile([P, S], U32, name="xw", tag="w1_g0", align_bytes=64)
         for lo, hi in ((FIRST, FIRST + 1), (0, 1), (1, LAST + 1)):
             nc.vector.tensor_copy(xw[:, CH * lo : CH * hi], xw_all[:].bitcast(U32).indirect(offsets[:, 8 * lo : 8 * hi]))
 

@@ -66,9 +66,10 @@ def tile_picked_yenkf_third_p_kernel(tc, x_words, x_scales, w1, obs, w2, ens, of
         for copy, piece, u, lo, hi in (
             (nc.scalar.copy, 0, 0, 0, 64),
             (nc.scalar.copy, 0, 1, 0, 64),
-            (nc.vector.tensor_copy, 1, 0, 64, 128),
-            (nc.scalar.copy, 1, 1, 64, 96),
-            (nc.vector.tensor_copy, 1, 1, 96, 128),
+            (nc.vector.tensor_copy, 1, 0, 64, 96),
+            (nc.scalar.copy, 1, 0, 96, 128),
+            (nc.vector.tensor_copy, 1, 1, 80, 128),
+            (nc.scalar.copy, 1, 1, 64, 80),
         ):
             first = W1_PIECES[piece][0]
             copy(
@@ -89,7 +90,6 @@ def tile_picked_yenkf_third_p_kernel(tc, x_words, x_scales, w1, obs, w2, ens, of
         obs_pair = keep.tile([P, 2 * VC, 4], F32, name="obs_pair", align_bytes=64)
         nc.gpsimd.tensor_scalar(obs_pair[:], obs_vt[:, 0 : 2 * VC, :], 1.0 / MEAN_FACTOR, 0.0, ALU.mult, ALU.add)
 
-        ens_first = keep.tile([P, 2, CH], F32, name="ens_first", align_bytes=64)
         mean_factor = keep.tile([P, 1], F32, name="mean_factor", tag="mean_factor", align_bytes=64)
         nc.gpsimd.memset(mean_factor[:], 1.0)
         nc.gpsimd.tensor_scalar(mean_factor[:], mean_factor[:], MEAN_FACTOR, 0.0, ALU.mult, ALU.add)
@@ -171,7 +171,6 @@ def tile_picked_yenkf_third_p_kernel(tc, x_words, x_scales, w1, obs, w2, ens, of
         def pick(dst, a, lo, hi):
             nc.scalar.activation(dst, ens_sb[a][:].indirect(offsets[:, 8 * lo : 8 * hi]), ACT.Copy)
 
-        pick(ens_first[:, 0, :], 0, FIRST, FIRST + 1)
         terms = [obs_pair[:].rearrange("p v t -> p (v t)")] + [pair[:, d, :] for d in range(D)]
         turned = psum.tile([P, P], F32, name="turned", tag="sum")
         for n, term in enumerate(terms):
@@ -181,11 +180,10 @@ def tile_picked_yenkf_third_p_kernel(tc, x_words, x_scales, w1, obs, w2, ens, of
         cen_pair = psum.tile([P, P], F32, name="cen_pair", tag="back")
         nc.tensor.transpose(cen_pair[:], turned_sb[:], ident[:])
 
-        pick(ens_first[:, 1, :], 1, FIRST, FIRST + 1)
-        ens_rest = keep.tile([P, 2, 3 * CH], F32, name="ens_rest", tag="mean_factor", align_bytes=64)
-        for lo, hi in ((LAST, LAST + 1), (0, 2)):
+        ens_g = keep.tile([P, 2, S], F32, name="ens_g", tag="mean_factor", align_bytes=64)
+        for lo in (2, 0):
             for a in range(2):
-                pick(ens_rest[:, a, CH * lo : CH * hi], a, lo, hi)
+                pick(ens_g[:, a, CH * lo : CH * (lo + 2)], a, lo, lo + 2)
 
         def quantise(name, rr, width):
             codes = keep.tile([P, width], U32, name="codes_" + name, align_bytes=64)
@@ -221,7 +219,7 @@ def tile_picked_yenkf_third_p_kernel(tc, x_words, x_scales, w1, obs, w2, ens, of
             nc.vector.tensor_tensor(
                 res[:].rearrange("p c (v d) -> p c v d", d=D),
                 z[:].rearrange("p c (d v) -> p c v d", d=D),
-                ens_rest[:, a, 0 : 2 * CH].rearrange("p (c v d) -> p c v d", c=2, d=D),
+                ens_g[:, a, 0 : 2 * CH].rearrange("p (c v d) -> p c v d", c=2, d=D),
                 ALU.add,
             )
             nc.sync.dma_start(outv[:, a, 0 : 2 * CH], res[:].rearrange("p c j -> p (c j)"))
@@ -261,7 +259,7 @@ def tile_picked_yenkf_third_p_kernel(tc, x_words, x_scales, w1, obs, w2, ens, of
         for a in range(2):
             for c in range(2):
                 second_product(z_pair[a][:, c, :], a, *mx_pair[c])
-        finish_chunk(FIRST, z_first, ens_first[:])
-        finish_chunk(LAST, z_last, ens_rest[:, :, CH * LAST : CH * (LAST + 1)])
+        finish_chunk(FIRST, z_first, ens_g[:, :, CH * FIRST : CH * (FIRST + 1)])
+        finish_chunk(LAST, z_last, ens_g[:, :, CH * LAST : CH * (LAST + 1)])
         for a in range(2):
             finish_pair(a, z_pair[a])

import concourse.mybir as mybir
from concourse.masks import make_identity

K, T, S, D, H, N = 512, 1024, 512, 8, 512, 256
V = S // D
P = 128
F32 = mybir.dt.float32
BF16 = mybir.dt.bfloat16
I32 = mybir.dt.int32
U32 = mybir.dt.uint32
U16 = mybir.dt.uint16
U8 = mybir.dt.uint8
X4 = mybir.dt.float8_e4m3fn_x4
ALU = mybir.AluOpType
ACT = mybir.ActivationFunctionType
AX = mybir.AxisListType
FLOPS = 2 * K * H * S + 2 * H * N * S
CH = 128
NCH = S // CH
VC = CH // D
GAIN = 0.3
W1_PIECES = ((0, 64), (64, 128))
FIRST, LAST = 3, 2
FIRST_SHARE = 5
MEAN_FACTOR = (1.0 - GAIN) / (GAIN * D)


def tile_picked_yenkf_third_p_kernel(tc, x_words, x_scales, w1, obs, w2, ens, offs, out):
    nc = tc.nc
    with (
        tc.tile_pool(name="keep", bufs=1) as keep,
        tc.psum_pool(name="psum", bufs=1) as psum,
    ):
        offsets = keep.tile([P, S // 16], U16, name="offsets")

        xs_all = keep.tile([P, T], U8, name="xs_all", align_bytes=64)
        nc.vector.memset(xs_all[:].bitcast(I32), 0)

        w1v = w1.rearrange("(p j) c -> p j c", j=4)
        w1_raw = []
        for lo, hi in W1_PIECES:
            raw = keep.tile([P, 4, 4 * (hi - lo)], F32, name="w1_raw%d" % lo, align_bytes=64)
            nc.sync.dma_start(raw[:], w1v[:, :, 4 * lo : 4 * hi])
            w1_raw.append(raw)
            if lo == 0:
                nc.sync.dma_start(offsets[:], offs)
                for q in range(4):
                    nc.sync.dma_start(xs_all[32 * q : 32 * q + 4, :].bitcast(I32), x_scales[0, 4 * q : 4 * q + 4, :].bitcast(I32))
        xw_all = keep.tile([P, T], I32, name="xw_all", align_bytes=64)
        nc.sync.dma_start(xw_all[:], x_words[0].rearrange("p n t -> p (n t)").bitcast(I32))
        obs_sb = keep.tile([P, 4, V], F32, name="obs_sb", align_bytes=64)
        ens_sb = [keep.tile([P, T], F32, name="ens_sb%d" % a, align_bytes=64) for a in range(2)]
        w2_raw = keep.tile([P, 4, N], F32, name="w2_raw", align_bytes=64)
        nc.sync.dma_start(w2_raw[:], w2.rearrange("(p j) c -> p j c", j=4))
        nc.sync.dma_start(obs_sb[:], obs.rearrange("(p t) v -> p t v", t=4))
        nc.sync.dma_start(ens_sb[0][:], ens[0:P, :])
        nc.sync.dma_start(ens_sb[1][:], ens[P : 2 * P, :])

        ident = keep.tile([P, P], F32, name="ident", align_bytes=64)
        make_identity(nc, ident[:])

        xs = keep.tile([P, S], U8, name="xs", align_bytes=64)
        nc.vector.tensor_copy(xs[:], xs_all[:].indirect(offsets[:]))

        w1_g = [keep.tile([P, 2, P, 4], BF16, name="w1_g%d" % u, tag="w1_g%d" % u, align_bytes=64) for u in range(2)]
        for copy, piece, u, lo, hi in (
            (nc.scalar.copy, 0, 0, 0, 64),
            (nc.scalar.copy, 0, 1, 0, 64),
            (nc.vector.tensor_copy, 1, 0, 64, 96),
            (nc.scalar.copy, 1, 0, 96, 128),
            (nc.vector.tensor_copy, 1, 1, 80, 128),
            (nc.scalar.copy, 1, 1, 64, 80),
        ):
            first = W1_PIECES[piece][0]
            copy(
                w1_g[u][:, :, lo:hi, :].rearrange("p t m j -> p m j t"),
                w1_raw[piece][:].rearrange("p j (m t) -> p m j t", t=4)[:, lo - first : hi - first, :, 2 * u : 2 * u + 2],
            )
        w1_c = keep.tile([P, H], U32, name="w1_c", align_bytes=64)
        w1_s = keep.tile([P, H], U8, name="w1_s", align_bytes=64)
        for u in range(2):
            cols = slice(H // 2 * u, H // 2 * (u + 1))
            nc.vector.quantize_mx(out=w1_c[:, cols].bitcast(X4), scales=w1_s[:, cols], in_=w1_g[u][:].rearrange("p t m j -> p (t m j)"))

        W = 4 * VC
        pair = keep.tile([P, D, 2 * W], F32, name="pair", align_bytes=64)
        anom_first = keep.tile([P, FIRST_SHARE, W], F32, name="anom_first", align_bytes=64)
        anom_last = keep.tile([P, 2, CH, 2], F32, name="anom_last", align_bytes=64)
        obs_vt = obs_sb[:].rearrange("p t v -> p v t")
        obs_pair = keep.tile([P, 2 * VC, 4], F32, name="obs_pair", align_bytes=64)
        nc.gpsimd.tensor_scalar(obs_pair[:], obs_vt[:, 0 : 2 * VC, :], 1.0 / MEAN_FACTOR, 0.0, ALU.mult, ALU.add)

        mean_factor = keep.tile([P, 1], F32, name="mean_factor", tag="mean_factor", align_bytes=64)
        nc.gpsimd.memset(mean_factor[:], 1.0)
        nc.gpsimd.tensor_scalar(mean_factor[:], mean_factor[:], MEAN_FACTOR, 0.0, ALU.mult, ALU.add)

        xw = keep.tile([P, S], U32, name="xw", tag="w1_g0", align_bytes=64)
        for lo, hi in ((FIRST, FIRST + 1), (0, 1), (1, LAST + 1)):
            nc.vector.tensor_copy(xw[:, CH * lo : CH * hi], xw_all[:].bitcast(U32).indirect(offsets[:, 8 * lo : 8 * hi]))

        def first_product(c, tiles):
            for t in range(4):
                nc.tensor.matmul_mx(
                    out=tiles[t],
                    lhsT=w1_c[:, P * t : P * (t + 1)].bitcast(X4),
                    lhsT_scale=w1_s[:, P * t : P * (t + 1)],
                    rhs=xw[:, CH * c : CH * (c + 1)].bitcast(X4),
                    rhs_scale=xs[:, CH * c : CH * (c + 1)],
                    start=True,
                    stop=True,
                )

        def by_member(bank):
            return bank[:].rearrange("p t (v d) -> p d v t", d=D)

        def anomalies(dst, bank, lo, hi):
            nc.scalar.activation(dst, by_member(bank)[:, lo:hi, :, :], ACT.Copy, scale=-GAIN)

        def reduce(dst, bank):
            nc.vector.tensor_reduce(dst, bank[:].rearrange("p t (v d) -> p t v d", d=D), AX.X, ALU.add)

        def centre(c, sums):
            made = keep.tile([P, VC, 4], F32, name="cen%d" % c, align_bytes=64)
            nc.vector.scalar_tensor_tensor(
                made[:],
                sums[:].rearrange("p t v -> p v t"),
                -(1.0 - GAIN) / D,
                obs_vt[:, VC * c : VC * (c + 1), :],
                ALU.mult,
                ALU.add,
            )
            return made

        y_first = psum.tile([P, 4, CH], F32, name="y_first", tag="first")
        first_product(FIRST, [y_first[:, t, :] for t in range(4)])
        anomalies(anom_first[:].rearrange("p d (v t) -> p d v t", t=4), y_first, 0, FIRST_SHARE)
        for c in range(2):
            y_pair = psum.tile([P, 4, CH], F32, name="y_pair%d" % c, tag="pair%d" % c)
            first_product(c, [y_pair[:, t, :] for t in range(4)])
            for lo, hi in ((0, D),) if c == 0 else ((0, D // 2), (D // 2, D)):
                anomalies(pair[:, lo:hi, W * c : W * (c + 1)].rearrange("p d (v t) -> p d v t", t=4), y_pair, lo, hi)
        y_last = [psum.tile([P, 2, CH], F32, name="y_last%d" % u, tag="last%d" % u) for u in range(2)]
        first_product(LAST, [y_last[t // 2][:, t % 2, :] for t in range(4)])

        w2_g = keep.tile([P, N, 4], BF16, name="w2_g", align_bytes=64)
        w2_c = keep.tile([P, N], U32, name="w2_c", align_bytes=64)
        w2_s = keep.tile([P, N], U8, name="w2_s", align_bytes=64)
        nc.vector.tensor_copy(
            w2_g[:].rearrange("p (c i) j -> p c j i", i=4),
            w2_raw[:].rearrange("p j (c i) -> p c j i", i=4),
        )
        sums_first = keep.tile([P, 4, VC], F32, name="sums_first", align_bytes=64)
        reduce(sums_first[:], y_first)
        nc.vector.quantize_mx(out=w2_c[:].bitcast(X4), scales=w2_s[:], in_=w2_g[:].rearrange("p c j -> p (c j)"))
        cen_first = centre(FIRST, sums_first)
        rr_first = keep.tile([P, D, W], BF16, name="rr_first", align_bytes=64)
        nc.gpsimd.tensor_tensor(
            rr_first[:, 0:FIRST_SHARE, :],
            anom_first[:],
            cen_first[:].rearrange("p v t -> p (v t)").unsqueeze(1).to_broadcast([P, FIRST_SHARE, W]),
            ALU.add,
        )

        sums_last = keep.tile([P, 4, VC], F32, name="sums_last", align_bytes=64)
        last_halves = [anom_last[:, u, :, :].rearrange("p (d v) t -> p d v t", d=D) for u in range(2)]
        anomalies(last_halves[0], y_last[0], 0, D)
        for u in (1, 0):
            reduce(sums_last[:, 2 * u : 2 * u + 2, :], y_last[u])
        anomalies(last_halves[1], y_last[1], 0, D)

        def pick(dst, a, lo, hi):
            nc.scalar.activation(dst, ens_sb[a][:].indirect(offsets[:, 8 * lo : 8 * hi]), ACT.Copy)

        terms = [obs_pair[:].rearrange("p v t -> p (v t)")] + [pair[:, d, :] for d in range(D)]
        turned = psum.tile([P, P], F32, name="turned", tag="sum")
        for n, term in enumerate(terms):
            nc.tensor.matmul(turned[:], term, ident[:], start=(n == 0), stop=(n == D), is_transpose=True)
        turned_sb = keep.tile([P, P], F32, name="turned_sb", align_bytes=64)
        nc.scalar.activation(turned_sb[:], turned[:], ACT.Copy, scale=mean_factor[:])
        cen_pair = psum.tile([P, P], F32, name="cen_pair", tag="back")
        nc.tensor.transpose(cen_pair[:], turned_sb[:], ident[:])

        ens_g = keep.tile([P, 2, S], F32, name="ens_g", tag="mean_factor", align_bytes=64)
        for lo in (2, 0):
            for a in range(2):
                pick(ens_g[:, a, CH * lo : CH * (lo + 2)], a, lo, lo + 2)

        def quantise(name, rr, width):
            codes = keep.tile([P, width], U32, name="codes_" + name, align_bytes=64)
            scales = keep.tile([P, width], U8, name="scales_" + name, align_bytes=64)
            nc.vector.quantize_mx(out=codes[:].bitcast(X4), scales=scales[:], in_=rr[:].rearrange("p d w -> p (d w)"))
            return codes, scales

        def second_product(dst, a, codes, scales):
            nc.tensor.matmul_mx(
                out=dst,
                lhsT=w2_c[:, P * a : P * (a + 1)].bitcast(X4),
                lhsT_scale=w2_s[:, P * a : P * (a + 1)],
                rhs=codes[:].bitcast(X4),
                rhs_scale=scales[:],
                start=True,
                stop=True,
            )

        outv = out.rearrange("(a p) j -> p a j", p=P)

        def finish_chunk(c, z, picked):
            res = keep.tile([P, 2, CH], F32, name="res%d" % c, tag="rr_last" if c == FIRST else "res", align_bytes=64)
            nc.vector.tensor_tensor(
                res[:].rearrange("p a (v d) -> p a v d", d=D),
                z[:].rearrange("p a (d v) -> p a v d", d=D),
                picked.rearrange("p a (v d) -> p a v d", d=D),
                ALU.add,
            )
            nc.sync.dma_start(outv[:, :, CH * c : CH * (c + 1)], res[:])

        def finish_pair(a, z):
            res = keep.tile([P, 2, CH], F32, name="res_pair%d" % a, align_bytes=64)
            nc.vector.tensor_tensor(
                res[:].rearrange("p c (v d) -> p c v d", d=D),
                z[:].rearrange("p c (d v) -> p c v d", d=D),
                ens_g[:, a, 0 : 2 * CH].rearrange("p (c v d) -> p c v d", c=2, d=D),
                ALU.add,
            )
            nc.sync.dma_start(outv[:, a, 0 : 2 * CH], res[:].rearrange("p c j -> p (c j)"))

        for d in range(FIRST_SHARE, D):
            nc.vector.scalar_tensor_tensor(
                rr_first[:, d, :].rearrange("p (v t) -> p v t", t=4),
                by_member(y_first)[:, d, :, :],
                -GAIN,
                cen_first[:],
                ALU.mult,
                ALU.add,
            )
        cen_last = centre(LAST, sums_last)
        z_first = psum.tile([P, 2, CH], F32, name="z_first", tag="sum")
        mx_first = quantise("first", rr_first, CH)
        for a in range(2):
            second_product(z_first[:, a, :], a, *mx_first)
        rr_last = keep.tile([P, D, W], BF16, name="rr_last", tag="rr_last", align_bytes=64)
        nc.gpsimd.tensor_tensor(
            rr_last[:].rearrange("p d w -> p (d w)"),
            anom_last[:].rearrange("p u c t -> p c u t"),
            cen_last[:].rearrange("p v t -> p (v t)").unsqueeze(1).to_broadcast([P, D, W]),
            ALU.add,
        )
        rr_pair = [keep.tile([P, D, W], BF16, name="rr_pair%d" % c, align_bytes=64) for c in range(2)]
        for c in range(2):
            cols = slice(W * c, W * (c + 1))
            nc.vector.tensor_tensor(rr_pair[c][:], pair[:, :, cols], cen_pair[:, cols].unsqueeze(1).to_broadcast([P, D, W]), ALU.add)

        z_last = psum.tile([P, 2, CH], F32, name="z_last", tag="last0")
        mx_last = quantise("last", rr_last, CH)
        for a in range(2):
            second_product(z_last[:, a, :], a, *mx_last)
        mx_pair = [quantise("pair%d" % c, rr_pair[c], CH) for c in range(2)]
        z_pair = [psum.tile([P, 2, CH], F32, name="z_pair%d" % a, tag="pair%d" % a) for a in range(2)]
        for a in range(2):
            for c in range(2):
                second_product(z_pair[a][:, c, :], a, *mx_pair[c])
        finish_chunk(FIRST, z_first, ens_g[:, :, CH * FIRST : CH * (FIRST + 1)])
        finish_chunk(LAST, z_last, ens_g[:, :, CH * LAST : CH * (LAST + 1)])
        for a in range(2):
            finish_pair(a, z_pair[a])
